import numpy as np, ml_dtypes
CORES = [16,17,18,19,32,33,34,35]
N = 8
BF = ml_dtypes.bfloat16
V, L, K, RO, KM = 4096, 128, 32, 3, 3967
B = L // N
WT = np.array([1, 7, 2, 6, 3, 5, 4, 4, 5, 3, 6, 2, 7, 1, 8, 1], np.int64)
def mix(v):
    return np.add.reduce(v * WT[:, None], axis=-2)
def spots(u, kap, a):
    return ((u * u >> 5)[..., None, :] + kap[..., None] * u[..., None, :] + a[..., None, None]) & (V - 1)
def first(x, z, kap, a=0):
    h = spots(mix(z), kap, np.asarray(a, np.int64)); e = np.add.reduce(np.abs(x[:, h] - z[:, None, :]), axis=0); m = np.argmin(e, axis=0)[None]
    return np.take_along_axis(h, m, 0)[0], np.take_along_axis(e, m, 0)[0]
def back(x, t, s):
    node = t[np.maximum(np.argsort(t)[s] - 1 - (1 + (mix(x[:, s]) & 15)) * np.arange(K)[:, None], 0)]
    e = np.add.reduce(np.abs(x[:, node] - x[:, None, s]), axis=0)
    return np.take_along_axis(node, np.argmin(e, axis=0)[None], 0)[0]
def far(rng):
    q = int(rng.integers(80, 113)); a = q // 2 + rng.integers(-7, 8, (8, L)); z = np.concatenate([a, q - a]); z[0] -= rng.integers(0, 4, L)
    return rng.integers(0, 8, (16, V)), z
def apart(rng, kap):
    z = rng.integers(2, 62, (16, L)); z[0] ^= 1 - (mix(z) & 1)
    h = spots(mix(z), kap, np.zeros((), np.int64)); used = np.zeros(V, bool); s = np.zeros(L, np.int64)
    for l in range(L):
        c = h[:, l]; s[l] = c[int(np.argmin(used[c]))]; used[s[l]] = True
    us, i = np.unique(s, return_index=True); k = len(us); rest = rng.permutation(np.flatnonzero(~used)); n = rest[:k]; rest = rest[k:]
    x = rng.integers(0, 64, (16, V)); x[:, us] = z[:, i] + rng.integers(-1, 2, (16, k)); x[:, n] = z[:, i] + 4 * rng.integers(0, 2, (16, k)) - 2
    o = rng.permutation(k); j = int(rng.integers(0, len(rest) // 2)); two = np.stack([n[o], us[o]], axis=1).reshape(-1)
    return x, z, np.concatenate([rest[:j], two, rest[j:]])
def parts(rng):
    x = rng.integers(0, 64, (N, 8, 16, V)); z = rng.integers(0, 64, (N, 8, 16, L)); ts = np.argsort(rng.random((N, 8, V)), axis=-1)
    return x, z, ts, rng.integers(0, KM + 1, (N, 8, 16)), rng.integers(20, 261, (N, 8))
def pack(x, z, ts, kap, th):
    return {"xr": np.ascontiguousarray(x.reshape(N, 128, V)).astype(np.float32).astype(BF), "ts": np.ascontiguousarray(ts).astype(np.int32), "zq": np.ascontiguousarray(z.reshape(N, 128, L)).astype(np.float32).astype(BF),
            "kap": np.ascontiguousarray(kap.reshape(N, 128, 1)).astype(np.int32), "th": np.ascontiguousarray(th.reshape(N, 8, 1)).astype(np.int32)}
def plant(rng, x, z, kap):
    h = spots(mix(z), kap, np.zeros((N, 8), np.int64)); m = rng.integers(0, 16, (N, 8, 1, L)); h = np.take_along_axis(h, m, 2)[:, :, 0]
    for r in range(N):
        for g in range(8):
            w = np.flatnonzero(rng.random(L) < rng.choice(np.array([0.2, 0.4, 0.6]))); c = int(rng.integers(2, 14))
            x[r, g][:, h[r, g, w]] = np.clip(z[r, g][:, w] + rng.integers(-c, c + 1, (16, len(w))), 0, 63)
def setup_inputs(rng):
    x, z, ts, kap, th = parts(rng)
    src = np.where(rng.random((N, 8, L)) < 0.12, rng.integers(0, L, (N, 8, L)), np.arange(L))
    z = np.take_along_axis(z, src[:, :, None, :], 3)
    plant(rng, x, z, kap)
    return pack(x, z, ts, kap, th)
def setup_inputs_corners(rng):
    x, z, ts, kap, th = parts(rng)
    for r in range(N):
        for g in range(8):
            y = (g + r) & 7
            if y == 0 and r & 1:
                x[r, g], z[r, g] = far(rng); X, Z = x[r, g], z[r, g]; s, e = first(X, Z, kap[r, g])
                v = np.abs(Z - X[:, back(X, ts[r, g], s)])[:, r * B:r * B + B]; e2 = first(X, v, kap[r, g], L)[1]
                th[r, g] = max(0, min(int(e2[int(rng.integers(0, B))]) - L, int(np.min(e)) - 1))
            elif y < 2:
                x[r, g, 0] &= 62; z[r, g, 0] |= 1; th[r, g] = 0
                if y == 1:
                    l = (0, L - 1)[int(rng.integers(0, 2))]; h = spots(mix(z[r, g]), kap[r, g], np.zeros((), np.int64))
                    x[r, g][:, h[int(rng.integers(0, 16)), l]] = z[r, g][:, l]
            elif y == 2: x[r, g], z[r, g], ts[r, g] = apart(rng, kap[r, g]); th[r, g] = 1008
            elif y == 3 and r & 1:
                x[r, g], z[r, g] = far(rng); c = np.bincount(first(x[r, g], z[r, g], kap[r, g])[1], minlength=1010)
                o = np.arange(513 + (r & 2), 1008, 4); th[r, g] = o[int(np.argmax(np.minimum(c[o], c[o + 1])))]
            elif y == 3: th[r, g] = np.sort(first(x[r, g], z[r, g], kap[r, g])[1])[L // 2]
            elif y < 6:
                us = rng.permutation(np.unique(first(x[r, g], z[r, g], kap[r, g])[0])); rest = rng.permutation(np.setdiff1d(np.arange(V), us))
                ts[r, g] = np.concatenate([us, rest] if y == 4 else [rest, us]); th[r, g] = 1008 if y == 4 else 600
            elif y == 6:
                x[r, g, 0] = 0; t = 15 * rng.integers(0, 2, V); x[r, g, 0] = ((t - mix(x[r, g])) & 15) + 16 * rng.integers(0, 4, V)
            else:
                pat = rng.integers(0, 64, (16, 3)); x[r, g] = pat[:, rng.integers(0, 3, V)]; z[r, g] = 63 * rng.integers(0, 2, (1, L)); z[r, g][:, L - 1] = 0; z[r, g][:, 0] = 63
    return pack(x, z, ts, kap, th)
def setup_inputs_crowd(rng):
    x, z, ts, kap, th = parts(rng); zero = np.zeros((), np.int64)
    for r in range(N):
        for g in range(8):
            X, Z = x[r, g], z[r, g]
            if g < 3:
                b = rng.integers(0, 16, 16); v = np.repeat(b[:, None], L, axis=1)
                for i, j in ((0, 13), (1, 12), (2, 11), (3, 10), (4, 9), (5, 8), (6, 7)):
                    fl = rng.random(L) < 0.5; v[i] = np.where(fl, b[j], b[i]); v[j] = np.where(fl, b[i], b[j])
                h = spots(mix(v), kap[r, g], zero)[:, 0]; X[:, h] = rng.integers(40, 64, (16, 16))
                X[:, h[int(rng.integers(0, 16))]] = np.clip(b + rng.integers(-2, 3, 16), 0, 63)
                odd = Z[:, 0].copy(); Z[:] = v; th[r, g] = (1008, 700, 350)[(g + r) % 3]
                if g == 1: Z[:, L - 1] = odd
                if g == 2: Z[:, 0] = odd
            elif g < 5:
                b = rng.integers(16, 44, 16); zi = b[:, None] + rng.integers(-2, 3, (16, 8)); hs = spots(mix(zi), kap[r, g], zero)[int(rng.integers(0, 16))]
                v = zi + rng.integers(-3, 4, (16, 8)); v[0] = v[0] + ((15 - mix(v)) & 15); X[:, hs] = v
                us = rng.permutation(np.unique(hs)); rest = rng.permutation(np.setdiff1d(np.arange(V), us)); a = rest[0]; X[:, a] = b
                at = 2 * np.arange(1, len(us) + 1); free = np.ones(V, bool); free[at] = False; free[0] = False
                ts[r, g, 0] = a; ts[r, g, at] = us; ts[r, g, free] = rest[1:]
                odd = Z[:, 0].copy(); Z[:] = zi[:, np.arange(L) & 7]; th[r, g] = (1008, 200)[(g + r) & 1]
                if g == 4: Z[:, 0] = odd
            elif g < 7:
                X[0] &= 62; Z[0] |= 1; th[r, g] = 0; odd = Z[:, L - 1].copy(); Z[:] = Z[:, :1].copy()
                if g == 6:
                    Z[:, L - 1] = odd; X[:, spots(mix(Z), kap[r, g], zero)[int(rng.integers(0, 16)), L - 1]] = odd
            else: Z[:] = Z[:, rng.integers(0, 4, L)].copy(); th[r, g] = 500
    return pack(x, z, ts, kap, th)
def setup_inputs_ends(rng):
    x, z, ts, kap, th = parts(rng); sh = np.array([1.0, 0.0, 0.5, 0.5, 0.9, 0.1, 0.5, 0.5]).reshape(1, 8, 1, 1)
    x = 63 * np.where(rng.random((N, 8, 1, V)) < sh, rng.integers(0, 2, (N, 8, 1, V)), rng.integers(0, 2, (N, 8, 16, V)))
    z = 63 * np.where(rng.random((N, 8, 1, L)) < sh, rng.integers(0, 2, (N, 8, 1, L)), rng.integers(0, 2, (N, 8, 16, L)))
    z[..., 0] = 63; z[..., 1] = 0; z[..., L - 2] = 0; z[..., L - 1] = 63
    kap = KM * rng.integers(0, 2, (N, 8, 16)); kap[..., 13] = 0; kap[..., 14] = KM; kap[..., 15] = 3841
    th = 1008 * rng.integers(0, 2, (N, 8)); th[:, 6] = 0; th[:, 7] = 1008
    c = (4095 * 4095 >> 5) & (V - 1); cs = np.array([c, (c + KM * 4095) & (V - 1), V - 1])
    for r in range(N):
        for g in range(8):
            y = (g + r) & 3; X = x[r, g]; X[:, cs] = (0, 63, 0, 0)[y]
            if y == 1: kap[r, g, 0] = 3841
            if y == 0: ts[r, g] = np.arange(V); X[:, V - 1] = 63
            elif y == 2: ts[r, g] = np.arange(V)[::-1]; X[:, 0] = 63
            else:
                i = int(np.flatnonzero(ts[r, g] == V - 1)[0]); j = V - 1 if y == 1 else 0; t = int(ts[r, g, j]); ts[r, g, j] = V - 1; ts[r, g, i] = t; X[:, V - 1] = 63
            if y < 2: X[:, ts[r, g, V - 2 - 16 * np.arange(K)]] = 63 * y
    X = x[N - 1, 1]; X[:] = np.where(rng.random((1, V)) < 0.1, 63 * rng.integers(0, 2, (16, V)), 0); X[0] = 0; X[:, cs] = 0
    z[N - 1, 1, 0] = 63; th[N - 1, 1] = 0
    return pack(x, z, ts, kap, th)
def setup_inputs_spread(rng):
    x, z, ts, kap, th = parts(rng)
    def odd(n):
        v = np.minimum((np.exp2(6 * rng.random((N, 8, 1, n))) * rng.random((N, 8, 16, n))).astype(np.int64), 63)
        return np.where(rng.random((N, 8, 1, n)) < 0.4, 63 - v, v)
    kap = np.minimum(np.exp2(12 * rng.random((N, 8, 16))).astype(np.int64) - 1, KM); th = np.minimum(np.exp2(10 * rng.random((N, 8))).astype(np.int64) - 1, 1008)
    return pack(odd(V), odd(L), ts, kap, th)
def setup_inputs_ties(rng):
    x, z, ts, kap, th = parts(rng); pat = rng.integers(0, 64, (N, 8, 16, 8))
    x = np.take_along_axis(pat, rng.integers(0, 8, (N, 8, 1, V)), 3); z = np.take_along_axis(pat, rng.integers(0, 8, (N, 8, 1, L)), 3)
    z = np.clip(z + rng.integers(-1, 2, z.shape) * (rng.random((N, 8, 1, L)) < 0.5), 0, 63); th = rng.integers(0, 40, (N, 8)); th[:, 3] = 0
    for r in range(N):
        for g in range(6):
            o = np.arange(V); ts[r, g] = o if g < 2 else o[::-1] if g < 4 else np.roll(o, int(rng.integers(1, V)))
    return pack(x, z, ts, kap, th)
def check_inputs(d):
    bad = []
    for k, lo, hi in (("xr", 0, 63), ("ts", 0, V - 1), ("zq", 0, 63), ("kap", 0, KM), ("th", 0, 1008)):
        a = np.asarray(d[k]).astype(np.float64)
        if not (np.min(a) >= lo and np.max(a) <= hi): bad.append("range of " + k)
        if np.any(a != np.floor(a)): bad.append("whole numbers of " + k)
    if np.any(np.sort(np.asarray(d["ts"]), axis=-1) != np.arange(V)): bad.append("permutation of ts")
    return bad
def reference(xr, ts, zq, kap, th):
    pick = np.take_along_axis
    X = xr.astype(np.float32).astype(np.int32).reshape(N, 8, 16, V); z = zq.astype(np.float32).astype(np.int32).reshape(N, 8, 16, L)
    T = ts.astype(np.int64); ka = kap.astype(np.int64).reshape(N, 8, 16); lim = th.astype(np.int64).reshape(N, 8); A = np.zeros((N, 8), np.int64)
    for rnd in range(RO):
        h = spots(mix(z), ka, A)
        xh = pick(X, h.reshape(N, 8, 1, 16 * L), 3).reshape(N, 8, 16, 16, L)
        e = np.add.reduce(np.abs(xh - z[:, :, :, None, :]), axis=2); m = np.argmin(e, axis=2)[:, :, None]
        s = pick(h, m, 2)[:, :, 0]; es = pick(e, m, 2)[:, :, 0]; xs = pick(X, s[:, :, None, :], 3)
        p = pick(np.argsort(T, axis=-1), s, 2); d = 1 + (mix(xs) & 15)
        at = np.maximum(p[:, :, None, :] - 1 - d[:, :, None, :] * np.arange(K)[:, None], 0)
        node = pick(T, at.reshape(N, 8, K * L), 2)
        xm = pick(X, node[:, :, None, :], 3).reshape(N, 8, 16, K, L)
        e = np.add.reduce(np.abs(xm - xs[:, :, :, None, :]), axis=2); k = np.argmin(e, axis=2)[:, :, None]
        n = pick(node.reshape(N, 8, K, L), k, 2)[:, :, 0]; xn = pick(X, n[:, :, None, :], 3)
        hit = es <= (lim + A)[:, :, None]
        vn = np.clip(xn + np.clip(z - xs, -2, 2), 0, 63); vs = (xs + z) >> 1
        z = np.where(hit[:, :, None, :], (z + xn) >> 1, np.abs(z - xn))
        for r in range(N):
            for g in range(8):
                lanes = np.flatnonzero(hit[r, g])
                un, i = np.unique(n[r, g, lanes], return_index=True); X[r, g][:, un] = vn[r, g][:, lanes[i]]
                us, i = np.unique(s[r, g, lanes], return_index=True); X[r, g][:, us] = vs[r, g][:, lanes[i]]
                gone = np.zeros(V, bool); gone[us] = True; old = T[r, g]
                T[r, g] = np.concatenate([old[~gone[old]], s[r, g, np.sort(lanes[i])]])
        A = L - np.add.reduce(hit.astype(np.int64), axis=2)
        z = np.ascontiguousarray(z.reshape(N, 8, 16, N, B).transpose(3, 1, 2, 0, 4)).reshape(N, 8, 16, L)
    return {"yx": X.reshape(N, 128, V).astype(np.float32).astype(BF), "yt": T.astype(np.float32), "yz": z.reshape(N, 128, L).astype(np.float32).astype(BF)}

@@ -1,0 +1,705 @@
+import numpy as np
+from concourse.bass import DstId, RemoteDMATransfer
+from concourse.mybir import AluOpType as A, AxisListType, ActivationFunctionType as F
+
+V, W = 4096, 4224
+f32, bf, f16, i32, u16 = "float32", "bfloat16", "float16", "int32", "uint16"
+R = np.s_
+SCRATCH, SHAPE, GROUP = {}, {}, {}
+
+
+def _decl(dtype, shape, names, where="sbuf"):
+    for n in names.split():
+        SCRATCH[n] = (where, [128] + shape, dtype)
+        SHAPE[n] = (shape, dtype, where)
+
+
+def _group(name, dtype, width, names):
+    names = names.split()
+    SCRATCH[name] = ("sbuf", [128, len(names), width], dtype)
+    for k, n in enumerate(names):
+        GROUP[n] = (name, k)
+        SHAPE[n] = ([width], dtype, "sbuf")
+
+
+_decl(bf, [W], "X")
+_decl(f32, [W], "XP XA XB POS")
+_decl(f32, [V], "VAL")
+_decl(bf, [V], "D")
+_decl(bf, [32, 128], "AB")
+_decl(bf, [512], "REP")
+_decl(bf, [128], "z0 land0 land1 land2 send0 send1 send2 xs")
+_decl(u16, [32], "oZ")
+_group("gb", bf, 128, "zt pd pds pdn ad sg c2 v160 vs xn192 xn0 vt vn first fm fn "
+                      "M16 BO ID NI HI I512 ONE HP NO1 NG C288 NM WBp WBn RS RP NS0 TGE TLT MA MB MC")
+_decl(bf, [8, 128], "LW SELG EQ GT")
+_group("gc", bf, 256, "RUF RX wh sega")
+_decl(bf, [768], "TW TQ")
+_decl(bf, [512], "VB")
+_decl(bf, [144], "Z1 Z2")
+_decl(bf, [8, 240], "A0 A1")
+_decl(bf, [8, 264], "SC")
+_decl(bf, [264], "IOC")
+_decl(bf, [8], "WQ")
+_group("gh", f16, 128, "um Pm Um Fm I239")
+_group("gf", f32, 128, "I32 CU1 CU2 C2K CT PRD KAP uu ku Kt nd na g1 wv v1 pk pT tv nv pv S0 DM tmp tm2")
+_group("gg", f32, 256, "CD CN C2A sm sn RST RSC KA KS seg segf Wf")
+_decl(f32, [8, 16], "PA PB")
+_decl(f32, [128], "CKC")
+_decl(f32, [8, 32], "M Mt")
+_decl(f32, [64], "IO CM")
+_group("ge", f32, 8, "col LC sW slT slN RT0 RT1 tc ntc Q32 thq wq cc ac th mv")
+_group("gi", i32, 128, "mi q0 sum ti tr r2")
+_decl(i32, [8, 16], "h")
+_decl(i32, [2, 128], "L")
+_group("gj", i32, 8, "thr thb kapi ki kj")
+_decl(u16, [256], "Wu oN oR")
+_decl(u16, [128], "oC")
+_decl(u16, [16], "oS oT su pu")
+_decl(f32, [512], "pA pB pC pD pE pK pS0 pS1", "psum")
+SEMAPHORES = ["sV", "sS", "sP", "sG", "sent", "arr0", "arr1", "arr2"] + ["d%d" % k for k in range(16)]
+LOADS, TURNS, SHAKE = 7, 1500, 5.0
+STEP_S, STEP_V, STEP_P, HALF = 1, 1, 2, 1
+SCR, NGR = 0, 8
+CY, PE, GA, SCA, WAKE = 1.04e-3, 0.52e-3, 1.56, 3.5, 0.1
+SGR = 4
+PACK_S, FIRST_S, MOVE_S, LAST_S = 1, 6, 12, 12
+
+
+def masks(topo, src, cores):
+    far = [c for c in cores if topo.chip(c) != topo.chip(src)]
+    near = [c for c in cores if c != src and c not in far]
+    fe = topo.engines(src, far[0])
+    ne = [e for e in topo.engines(src, near[0]) if e not in fe]
+    out = {}
+    for dsts, eng in ((far, fe), (near, ne)):
+        share = [1] * len(dsts)
+        k = 0
+        while sum(share) + share[k % len(dsts)] <= len(eng):
+            share[k % len(dsts)] *= 2
+            k += 1
+        at = 0
+        for c, n in zip(dsts, share):
+            out[c] = eng[at:at + n]
+            at += n
+    return out
+
+
+def depend(ops):
+    acc, last, out = {}, {}, []
+    for n, o in enumerate(ops):
+        hard, soft = set(), set()
+        for name, lo, hi in o["r"]:
+            for m, l2, h2, wr in acc.get(name, []):
+                if wr and l2 <= hi and lo <= h2:
+                    hard.add(m)
+        for name, lo, hi in o["w"]:
+            keep = []
+            for m, l2, h2, wr in acc.get(name, []):
+                if l2 <= hi and lo <= h2:
+                    hard.add(m)
+                if not (lo <= l2 and h2 <= hi):
+                    keep.append((m, l2, h2, wr))
+            acc[name] = keep
+        for bank in o["x"]:
+            if bank in last:
+                (soft if ops[last[bank]]["e"] == o["e"] else hard).add(last[bank])
+            last[bank] = n
+        for name, lo, hi in o["r"]:
+            acc.setdefault(name, []).append((n, lo, hi, False))
+        for name, lo, hi in o["w"]:
+            acc[name].append((n, lo, hi, True))
+        hard.discard(n)
+        soft.discard(n)
+        out.append((hard, soft - hard))
+    return out
+
+
+ORDER = {}
+
+
+def arrange(ops):
+    n = len(ops)
+    if n in ORDER:
+        return [ops[k] for k in ORDER[n]]
+    dep = depend(ops)
+    pre = [[(m, WAKE + ops[m]["lat"]) for m in d[0]] + [(m, 0.0) for m in d[1]] for d in dep]
+    for k in range(1, LOADS):
+        pre[k].append((k - 1, 0.0))
+    seen = {}
+    for k, o in enumerate(ops):
+        if o["tag"]:
+            if (o["tag"], o["e"]) in seen:
+                pre[k].append((seen[o["tag"], o["e"]], 0.0))
+            seen[o["tag"], o["e"]] = k
+    succ = [[] for _ in ops]
+    for k in range(n):
+        for m, lag in pre[k]:
+            succ[m].append((k, lag))
+    c, eng = [o["c"] for o in ops], [o["e"] for o in ops]
+
+    def place(order, before, first):
+        busy, at = {e: [] for e in "VSPGY"}, [0.0] * n
+        for k in order:
+            t = max([at[m] + c[m] + lag for m, lag in before[k]] + [first[k]])
+            b = busy[eng[k]]
+            j = len(b)
+            while j and b[j - 1][1] > t:
+                j -= 1
+            while j < len(b) and b[j][0] < t + c[k]:
+                t = max(t, b[j][1])
+                j += 1
+            b.insert(j, (t, t + c[k]))
+            at[k] = t
+        return at
+    lat, zero = [o["lat"] for o in ops], [0.0] * n
+    way = [0.0] * n
+    for k in range(n - 1, -1, -1):
+        way[k] = c[k] + max([way[s] + lag for s, lag in succ[k]] + [lat[k]])
+    best, seed = None, 1
+    for turn in range(TURNS):
+        if turn % 3 == 0:
+            key = [-x for x in way] if best is None else list(best[2])
+            for k in range(n):
+                seed = (seed * 1103515245 + 12345) % 2 ** 31
+                key[k] = max([key[k] + (SHAKE * (seed / 2 ** 31) ** 4 if turn else 0.0)] + [key[m] + 1e-6 for m, lag in pre[k]])
+            order = sorted(range(n), key=lambda k: (key[k], k))
+        at = place(order, pre, zero)
+        end = max(at[k] + c[k] + lat[k] for k in range(n))
+        if best is None or end < best[0]:
+            best = (end, sorted(range(n), key=lambda k: (at[k], k)), at)
+        back = place(sorted(range(n), key=lambda k: (-at[k] - c[k], -k)), succ, lat)
+        order = sorted(range(n), key=lambda k: (-back[k] - c[k], k))
+    ORDER[n] = best[1]
+    ORDER["end"] = best[0]
+    return [ops[k] for k in best[1]]
+
+
+def emit(g, T, ops):
+    eng = {"V": g.vector, "S": g.scalar, "P": g.tensor, "G": g, "Y": g.sync}
+    known = {e: {} for e in eng}
+    clock, waits, need = {}, [], set()
+    for n, (o, (d, _)) in enumerate(zip(ops, depend(ops))):
+        kn = known[o["e"]]
+        ws = []
+        for m in sorted(d, reverse=True):
+            if kn.get(ops[m]["sem"] or ops[m]["e"], -1) >= m:
+                continue
+            ws.append(m)
+            need.add(m)
+            for c, x in clock[m].items():
+                kn[c] = max(kn.get(c, -1), x)
+        waits.append(ws)
+        clock[n] = {} if o["far"] else dict(kn)
+        clock[n][o["sem"] or o["e"]] = n
+    count, val = {}, {}
+    for n, o in enumerate(ops):
+        q = eng[o["e"]]
+        for m in waits[n]:
+            q.wait_ge(T.sem[val[m][0]], val[m][1])
+        ins = o["f"](q)
+        if o["sem"]:
+            val[n] = (o["sem"], o["n"])
+            count[o["sem"]] = o["n"]
+            if not o["far"]:
+                ins.then_inc(T.sem[o["sem"]], 16)
+        elif n in need:
+            s = "s" + o["e"]
+            count[s] = count.get(s, 0) + 1
+            val[n] = (s, count[s])
+            ins.then_inc(T.sem[s], 1)
+    for s, c in count.items():
+        g.wait_ge(T.sem[s], c)
+
+
+def rank_program(g, core, T, topo):
+    rank = T.rank_of(core)
+    if rank is None:
+        return
+    ops, ndma, tag = [], [0], [None]
+
+    def v(name, *idx, p=slice(None)):
+        shape, dtype, where = SHAPE[name]
+        if len(idx) == 1 and isinstance(idx[0], tuple):
+            idx = idx[0]
+        at = np.arange(int(np.prod(shape))).reshape(shape)[idx]
+        ap = T[GROUP[name][0]][(p, GROUP[name][1]) + (idx or (slice(None),))] if name in GROUP else T[name][(p,) + idx]
+        span = (name, int(np.min(at)), int(np.max(at)))
+        return {"ap": ap, "n": int(np.size(at)), "k": [span], "two": dtype in (bf, f16, u16), "ps": where == "psum", "f32": dtype == f32, "ind": False, "off": []}
+
+    def c1(name, k):
+        return v(name, R[k:k + 1])
+
+    def ind(name, off, width=W):
+        x = v(name, R[0:width])
+        return dict(x, ap=x["ap"].indirect(off["ap"]), n=16 * off["n"], ind=True, off=off["k"])
+
+    def u(x):
+        return v(x) if isinstance(x, str) else x
+
+    def raw(x):
+        return x["ap"] if isinstance(x, dict) else x
+
+    def op(e, f, outs, ins, c, sem=None, n=16, lat=0.0, far=False):
+        r, w, banks = [], [], set()
+        for x in [y for y in ins if isinstance(y, dict)] + outs:
+            r.extend(x["off"])
+            if x["ps"]:
+                banks.add(x["k"][0][0])
+            if not (x["ps"] and e == "P"):
+                (w if any(x is y for y in outs) else r).extend(x["k"])
+        ops.append({"e": e, "f": f, "r": r, "w": w, "x": sorted(banks), "tag": tag[0], "c": c, "sem": sem, "n": n, "lat": lat, "far": far})
+
+    def cost(e, out, a, per):
+        if out["ind"] or a["ind"]:
+            return 0.06 + a["n"] * (SCA if out["ind"] else GA) * CY
+        return max(64, a["n"] * per) * CY + (0.05 if e == "S" else 0.0)
+
+    def dma(e, out, in_, lat):
+        outs = [out] if isinstance(out, dict) else []
+        op(e, lambda q: q.dma_start(raw(out), raw(in_)), outs, [in_], 0.1, "d%d" % ndma[0], 16, lat)
+        ndma[0] += 1
+
+    def ms(out, c):
+        out = u(out)
+        op("V", lambda q: q.memset(out["ap"], c), [out], [], cost("V", out, out, 0.5 if out["two"] else 1))
+
+    def cp(out, a):
+        out, a = u(out), u(a)
+        op("V", lambda q: q.tensor_copy(out["ap"], a["ap"]), [out], [a], cost("V", out, a, 0.5 if out["two"] and a["two"] else 1))
+
+    def tt(out, a, b, o):
+        out, a, b = u(out), u(a), u(b)
+        op("V", lambda q: q.tensor_tensor(out["ap"], a["ap"], b["ap"], o), [out], [a, b], cost("V", out, a, 1 if a["ps"] or b["ps"] else 2))
+
+    def ts(out, a, s1, o0, s2=None, o1=None):
+        out, a = u(out), u(a)
+        args = (out["ap"], a["ap"], raw(s1), raw(s2), o0) + (() if o1 is None else (o1,))
+        op("V", lambda q: q.tensor_scalar(*args), [out], [a, s1, s2], cost("V", out, a, 0.5 if out["two"] and a["two"] else 1))
+
+    def red(out, a):
+        a = u(a)
+        op("V", lambda q: q.tensor_reduce(out["ap"], a["ap"], AxisListType.X, A.add), [out], [a], cost("V", out, a, 1))
+
+    def scan(out, a, b, init, o0, o1):
+        out, a, b = u(out), u(a), u(b)
+        op("V", lambda q: q.tensor_tensor_scan(out["ap"], a["ap"], b["ap"], init, o0, o1), [out], [a, b], cost("V", out, a, 1))
+
+    def act(out, a, fn=F.Identity, acc=None, **k):
+        out, a = u(out), u(a)
+        kw = {x: raw(y) for x, y in k.items()}
+        if acc:
+            kw["accum_out"] = acc["ap"]
+        op("S", lambda q: q.activation(out["ap"], a["ap"], fn, **kw), [out] + ([acc] if acc else []), [a] + list(k.values()), cost("S", out, a, 1))
+
+    def mm(out, *terms, st=True, sp=True):
+        for j, (l, rr) in enumerate(terms):
+            l, rr = u(l), u(rr)
+            a, b = st and j == 0, sp and j == len(terms) - 1
+            op("P", lambda q, l=l, rr=rr, a=a, b=b: q.matmul(out["ap"], l["ap"], rr["ap"], a, b), [out], [l, rr], max(64, rr["n"]) * (4 if l["f32"] else 1) * PE)
+
+    def iota(out, pat, base, cm=0):
+        out = u(out)
+        kw = {"allow_small_or_imprecise_dtypes": True} if out["two"] or out["f32"] else {}
+        op("G", lambda q: q.iota(out["ap"], pat, base, cm, **kw), [out], [], 0.13 + 2 * out["n"] * CY)
+
+    def sel(out, a, pat, o, base, cm, fill=0.0):
+        out, a = u(out), u(a)
+        op("G", lambda q: q.affine_select(out["ap"], a["ap"], pat, o, fill, base, cm), [out], [a], 0.17 + 2 * out["n"] * CY)
+
+    col = [c1("col", k) for k in range(8)]
+    Mc = [c1("M16", k) for k in range(4)]
+    Q = v("BO", R[0:128:16])
+
+    dma("Y", v("L", 0), T.ts[0:8:2, :], 2.3)
+    dma("S", v("L", 1), T.ts[1:8:2, :], 2.6)
+    dma("Y", v("z0"), T.zq[:], 2.7)
+    dma("S", c1("kapi", 0), T.kap[:], 2.7)
+    dma("S", v("thr", p=R[0:1]), T.th[:], 2.7)
+    dma("Y", v("X", R[0:2048]), T.xr[:, 0:2048], 5.0)
+    dma("Y", v("X", R[2048:V]), T.xr[:, 2048:V], 7.5)
+
+    iota("mi", [[0, 8], [-1, 16]], 128, 1)
+    iota("IO", [[1, 64]], 0)
+    for n, c in (("ONE", 1.0), ("CT", 0.0), ("HP", 0.5)):
+        ms(n, c)
+    for n, c in (("NO1", -1), ("CU1", -2048), ("C2K", 2048), ("C288", 288), ("CU2", -12448), ("Z1", 0), ("Z2", 0), ("tm2", 0)):
+        iota(n, [[0, v(n)["n"]]], c)
+    for n in ("X", "XA", "XB", "XP", "POS"):
+        iota(v(n, R[V:W]), [[0, W - V]], 0)
+    ms(c1("ac", 0), -0.375)
+    sel("tmp", "ONE", [[-16, 8], [0, 16]], A.is_ge, 0, 1)
+    sel("BO", "tmp", [[16, 8], [0, 16]], A.is_ge, 15, -1)
+    iota(v("CT", R[0:16:2]), [[1, 8]], 1)
+    iota(v("CT", R[1:14:2]), [[-1, 7]], 7)
+    sel("ID", "ONE", [[-1, 128]], A.is_equal, 0, 1)
+    ts("q0", "mi", 15, A.bitwise_and)
+    ts("M16", "q0", 0.0, A.is_equal)
+    ts(v("VAL", R[0:64]), "IO", Mc[1], A.mult, 128.0, A.add)
+    ts("CM", "IO", Mc[0], A.mult)
+    for k in (1, 2, 4):
+        ts(v("VAL", R[64 * k:128 * k]), v("VAL", R[0:64 * k]), c1("CM", k), A.add)
+    for t in range(1, 8):
+        ts(v("VAL", R[512 * t:512 * t + 512]), v("VAL", R[0:512]), c1("CM", 8 * t), A.add)
+    for g0 in range(2):
+        cp(v("M", R[:, 16 * g0:16 * g0 + 16]), v("L", g0))
+    for c in range(8):
+        a, b = v("Mt", c), v("M", c)
+        op("V", lambda q, a=a, b=b: q.transpose(a["ap"], b["ap"]), [a], [b], 64 * CY)
+        cp(v("Wu", R[c:256:8]), a)
+    for t in range(0, 16, STEP_P):
+        act(ind("POS", v("Wu", R[16 * t:16 * (t + STEP_P)]), V), v("VAL", R[256 * t:256 * (t + STEP_P)]), F.Silu)
+    for at, c in ((15, 1.0), (16, 64.0), (19, -66.0), (32, 2.0 ** -8), (33, 2.0 ** -14), (35, -65 * 2.0 ** -14), (48, 16384.0), (64, 64.0), (67, -82.0),
+                  (68, -1 / 128.0), (83, -16.0), (84, 1 / 128.0), (99, 12.0), (100, -15 / 4096.0)):
+        if c == int(c):
+            iota(c1("CT", at), [[0, 1]], int(c))
+        else:
+            ms(c1("CT", at), c)
+    iota(v("CT", R[17:19]), [[0, 2]], 1)
+    iota(v("CT", R[65:67]), [[0, 2]], 1)
+    iota(v("CT", R[113:128]), [[0, 15]], 128)
+    iota(c1("CT", 112), [[0, 1]], 192)
+    tt("PRD", "CT", "M16", A.mult)
+    for k in range(8):
+        red(col[k], v("PRD", R[16 * k:16 * k + 16]))
+    cp("I32", "ID")
+    cp(c1("cc", 0), c1("kapi", 0))
+    ts("tmp", "M16", c1("cc", 0), A.mult)
+    cp("S0", "BO")
+    mm(v("pD", R[0:128]), ("S0", "tmp"))
+    cp("KAP", v("pD", R[0:128]))
+    iota("CKC", [[16384, 2], [0, 8], [2048, 8]], -16711680)
+    a, b = v("thb"), v("thr", p=R[0:1])
+    op("G", lambda q, a=a, b=b: q.partition_broadcast(a["ap"], b["ap"], 128), [a], [b], 0.2)
+    ts("LC", v("IO", R[0:8]), Mc[3], A.mult, 2.0 ** -12, A.mult)
+    ts("LC", "LC", col[2], A.add)
+    cp("VB", v("VAL", R[0:512]))
+    ts(v("Z1", R[15:128:16]), Q, 32768.0, A.mult)
+    ts(v("Z2", R[15:128:16]), Q, -8192.0, A.mult)
+    for t in range(8):
+        ts(v("LW", t), "BO", c1("LC", t), A.mult)
+    for n, c in (("NI", -1.0), ("HI", 0.5), ("I512", 512.0), ("I239", 239.75)):
+        ts(n, "ID", c, A.mult)
+    for n, c in (("MA", -1664.0), ("MB", 2048.0), ("MC", 2560.0)):
+        ts(n, "M16", c, A.mult)
+    ts("NM", "M16", 4.0, A.mult, -4.0, A.add)
+    for n, k, c in (("WBp", 0, 1.0), ("WBn", 0, -1.0), ("RS", 1, 1.0), ("RP", 4, 1.0), ("S0", 3, 1.0), ("NS0", 3, -1.0), (v("RUF", R[0:128]), 5, 1.0),
+                    (v("RUF", R[128:256]), 6, 1.0), (v("RX", R[0:128]), 0, 1.0), (v("RX", R[128:256]), 0, 0.0625)):
+        ts(n, "BO", col[k], A.mult, c, A.mult)
+    ts("wq", Q, col[1], A.mult)
+    cp("WQ", "wq")
+    cp("Q32", Q)
+    for k in range(8):
+        ts(v("SELG", k), "ONE", c1("wq", k), A.mult)
+    for n, pk_, pq in (("TW", lambda s: [[4 * s, 8], [0, 8], [s, 4]], lambda s: [[0, 24], [s, 8], [0, 4]]),
+                       ("TQ", lambda s: [[0, 8], [s, 8], [8 * s, 4]], lambda s: [[0, 3], [s, 8], [0, 32]])):
+        for j, (s, base) in enumerate(((0, 1), (-1, 0), (16, 0))):
+            iota(v(n, R[256 * j:256 * j + 256]), pk_(s), base)
+        sel(n, n, pq(-16), A.is_ge, 0, 1)
+        sel(n, n, pq(16), A.is_ge, 15, -1)
+    iota("RST", [[0, 256]], 0)
+    sel("RSC", "RST", [[0, 16], [1, 16]], A.not_equal, 0, 0, 1e9)
+    sel("RST", "RST", [[0, 8], [1, 32]], A.not_equal, 0, 0, -1e9)
+    iota("r2", [[0, 8], [2, 16]], 0)
+    iota("IOC", [[1, 264]], -1)
+    iota("CD", [[4096, 2], [0, 128]], -4096, -1)
+    iota(v("CN", R[0:128]), [[0, 128]], 192 * 16384 - 4096, -1)
+    iota(v("CN", R[128:256]), [[0, 128]], -4096, -1)
+    iota("C2A", [[32, 256]], 0)
+    sel("TGE", "NO1", [[-1, 128]], A.is_ge, 0, 1)
+    sel("TLT", "ONE", [[1, 128]], A.is_gt, 0, -1)
+    sel("NG", "NO1", [[-1, 128]], A.not_equal, 0, 1, -32768.0)
+    iota(c1("cc", 2), [[0, 1]], 4096, 1)
+    for n in ("A0", "A1"):
+        for k in range(4):
+            iota(v(n, R[2 * k:2 * k + 2]), [[0, 480]], 0)
+    tt("thq", "thb", "Q32", A.mult)
+    red(c1("cc", 1), "thq")
+    ts(c1("th", 0), c1("cc", 1), 0.5, A.add)
+    ts(c1("th", 3), c1("cc", 1), 64.5, A.add)
+    ts("DM", "M16", c1("cc", 2), A.mult)
+    scan("PRD", "HP", "tm2", 2.0 ** 64, A.mult, A.add)
+    tt("tmp", "PRD", "I32", A.mult)
+    red(c1("cc", 3), "tmp")
+    tt(v("uu", R[0:16]), v("M16", R[0:16]), v("IO", R[0:16]), A.mult)
+    red(c1("cc", 6), v("uu", R[0:16]))
+    iota(v("ku", R[0:32]), [[16, 8], [0, 4]], 0)
+    ts("oZ", v("ku", R[0:32]), c1("cc", 6), A.add)
+    ts(c1("cc", 4), c1("cc", 6), 2.0, A.mult)
+    ts(c1("cc", 7), c1("cc", 2), 4096.0 + 16 * SCR, A.is_ge, 128.0, A.mult)
+    ts("C2A", "C2A", c1("cc", 4), A.add, c1("cc", 7), A.add)
+    cp(c1("mv", 0), col[7])
+    cp(c1("mv", 2), Mc[1])
+    cp(c1("mv", 3), Mc[2])
+
+    my = masks(topo, core, T.cores)
+    arrive = sum(len(masks(topo, c, T.cores)[core]) for c in T.cores if c != core)
+    XT = ["XA", "XB", "XA"]
+
+    def measure(c, win, off, bias, key, zz, last, end):
+        tag[0] = "measure"
+        for a, b in ((0, 5), (5, 8)) if HALF and end else ((0, 8),):
+            d = v("D", R[512 * c + 64 * a:512 * c + 64 * b])
+            tt(d, ind(win, v(off, R[32 * c + 4 * a:32 * c + 4 * b])), v("REP", R[64 * a:64 * b]), A.add)
+            act(v("AB", R[8 * (c // 2) + a:8 * (c // 2) + b, 64 * (c % 2):64 * (c % 2) + 64]), d, F.Abs, bias=bias)
+        tag[0] = None
+        if c % 2:
+            b = c // 2
+            mm(key, *[(v(zz, R[15 - r:143 - r]), v("AB", R[8 * b:8 * b + 8, r:128:16])) for r in range(16)], st=False, sp=last)
+
+    def reorder(src, dst, lst, on_s):
+        t = 0
+        while t < 16:
+            s = t >= 16 - on_s
+            k = min(STEP_S if s else STEP_V, (16 if s else 16 - on_s) - t)
+            tag[0] = "move"
+            (act if s else cp)(v(dst, R[256 * t:256 * (t + k)]), ind(src, v(lst, R[16 * t:16 * (t + k)])))
+            tag[0] = None
+            t += k
+
+    def cands(rd):
+        zb = "z0" if rd == 0 else "land%d" % (rd - 1)
+        sc, bi = (1.0, 0.0) if rd == 0 else (-1.0, -160.0)
+        ut = v("pA", R[0:128])
+        mm(ut, ("I32", "CU2" if rd else "CU1"), (zb, "WBn" if rd else "WBp"))
+        tt("um", ut, "M16", A.mult)
+        for b in ("pB", "pC"):
+            mm(v(b, R[0:128]), ("I32", "C2K"), ("um", "BO"))
+        keys = [v("pA", R[128:192]), v("pK", R[0:64])]
+        for b in range(2):
+            mm(keys[b], ("I32", v("CKC", R[64 * b:64 * b + 64])), sp=False)
+        act("REP", ind(zb, v("oZ"), 128), scale=-sc, bias=-bi)
+        act("zt", zb, scale=sc, bias=bi)
+        act("uu", v("pB", R[0:128]), F.Square)
+        tt(v("pC", R[128:256]), v("pC", R[0:128]), "KAP", A.mult)
+        ts("q0", "uu", 0.03125, A.mult, c1("ac", rd), A.add)
+        tt("sum", v("pC", R[128:256]), "q0", A.add)
+        ts("h", "sum", V - 1, A.bitwise_and)
+        for c in range(4):
+            cp(v("oC", R[32 * c:32 * c + 32]), v("h", R[:, 4 * c:4 * c + 4]))
+            measure(c, "X", "oC", 0.0, keys[c // 2], "Z1", True, c == 3 and rd > 0)
+        ts("PB", "h", -2048.0, A.add, 0.0, A.max)
+        ts("PA", "h", -2048.0, A.add, 0.0, A.min)
+        for b in range(2):
+            tt(v("KA", R[b:128:2]), keys[b], v("PA", R[:, 8 * b:8 * b + 8]), A.subtract)
+            tt(v("KA", R[128 + b:256:2]), keys[b], v("PB", R[:, 8 * b:8 * b + 8]), A.add)
+        scan("KS", "RSC", "KA", 0.0, A.add, A.min)
+        tt("sW", v("KS", R[143:256:16]), v("KS", R[15:128:16]), A.subtract)
+        ts(v("su", R[0:8]), "sW", 2048.0, A.add)
+
+    def spread(digits, cols):
+        for k in range(8):
+            mm(v("pS%d" % (k // 4), R[128 * (k % 4):128 * (k % 4) + 128]), (v("SELG", k), digits))
+        mm(v("pD", R[256:264]), (digits, "WQ"))
+        act(cols, v("pD", R[256:264]))
+
+    def compare(out, cols, k, how):
+        src = v("pS%d" % (k // 4), R[128 * (k % 4):128 * (k % 4) + 128])
+        if how == "eq":
+            ts(v(out, k), src, c1(cols, k), A.is_equal, 0.375, A.mult)
+        elif how == "gt":
+            ts(v(out, k), src, c1(cols, k), A.is_gt)
+        else:
+            act(v(out, k), src, F.Sign, scale=-1.0, bias=c1(cols, k))
+
+    def places(rd):
+        sl, P = v("su", R[0:8]), v("pA", R[0:128])
+        cp("xs", ind("X", sl))
+        act("pd", ind("POS", sl))
+        n1, n2, kn = v("pC", R[0:64]), v("pE", R[0:192]), v("pK", R[0:256])
+        tw = lambda j, a, b: v("TW", R[256 * j + a:256 * j + b])
+        tq = lambda j: v("TQ", R[256 * j:256 * j + 256])
+        mm(n1, ("MA", tw(2, 0, 64)), ("MB", tw(0, 0, 64)), sp=False)
+        mm(n2, ("MA", tw(2, 64, 256)), ("MB", tw(0, 64, 256)), sp=False)
+        mm(kn, ("MA", tq(2)), ("MC", tq(0)), sp=False)
+        if rd:
+            spread("pd", "slT")
+        mm(v("pB", R[0:256]), ("xs", "RX"), ("pd", "RUF"))
+        mm(P, ("pd", "RP"), sp=rd == 0)
+        if rd:
+            mm(v("pA", R[16 * SGR:128]), *[("HP", v("NO1", R[16 * SGR:128]))] * rd, st=False, sp=False)
+        act("REP", ind("xs", v("oZ"), 128), scale=-1.0, bias=192.0)
+        for s in range(rd):
+            buf = ("GT", "EQ")[s]
+            for k in range(8):
+                compare(buf, "RT%d" % s, k, "gt" if k < SGR else "sign")
+            for k in (0, 4, 1, 5, 2, 6, 3, 7):
+                mm(v("pA", R[16 * k:16 * k + 16]), (v(buf, k), v("NO1" if k < SGR else "HP", R[0:16])), st=False, sp=s == rd - 1 and k == 7)
+        tt("Um", v("pB", R[0:128]), "M16", A.mult)
+        tt("Fm", v("pB", R[128:256]), "M16", A.mult)
+        tt("Pm", P, "M16", A.mult)
+        mm(n1, ("Um", tw(1, 0, 64)), ("Fm", tw(2, 0, 64)), ("Pm", tw(0, 0, 64)), st=False)
+        mm(n2, ("Um", tw(1, 64, 256)), ("Fm", tw(2, 64, 256)), ("Pm", tw(0, 64, 256)), st=False)
+        mm(kn, ("Um", tq(1)), ("Fm", tq(2)), ("Pm", tq(0)), st=False, sp=False)
+        cp(v("oN", R[0:64]), n1)
+        cp(v("oN", R[64:256]), n2)
+        if rd == 0:
+            spread("pd", "slT")
+
+    def lowest(bank):
+        for k in range(8):
+            mm(v(bank, R[16 * k:16 * k + 16]), (v("EQ", k), v("wh", R[16 * k:16 * k + 16])))
+
+    def offsets(o, src, flag, buf, bank, n=2):
+        for j in range(n):
+            tt(v(buf, R[128 * j:128 * j + 128]), v(src, R[128 * j:128 * j + 128]), flag, A.mult)
+        for j in range(n):
+            mm(v(bank, R[8 * j:8 * j + 8]), ("DM", "Q32"), (v(buf, R[128 * j:128 * j + 128]), "Q32"))
+        cp(v(o, R[0:8 * n]), v(bank, R[0:8 * n]))
+
+    def match(rd):
+        a, b, c, d = (v(x, R[0:128]) for x in ("pA", "pB", "pC", "pD"))
+        act("pT", a)
+        mm(b, ("ID", "zt"), ("NI", "xs"))
+        mm(c, ("HI", "zt"), ("HI", "xs"))
+        act("ad", b, F.Abs)
+        ts("c2", b, -2.0, A.max, 2.0, A.min)
+        mm(a, ("BO", "ad"))
+        act("v160", c, bias=159.75)
+        act("sg", a, F.Sign, c1("cc", 5), scale=-1.0, bias=c1("th", rd))
+        act("vs", "v160", bias=-160.0)
+        mm(d, ("sg", "ID"))
+        mm(v("pD", R[128:256]), ("sg", "ID"), ("ID", "NM"))
+        mm(a, ("ID", "zt"), ("I239", "sg"))
+        mm(c, ("NI", "zt"), ("I512", "sg"))
+        act("wh", v("pD", R[0:256]), F.Relu, scale=c1("cc", 3))
+        act("Kt", a, F.Abs, bias=79.75)
+        act("nd", c, bias=352.0)
+        act("na", "sg", scale=0.25, bias=-0.75)
+        act("pds", ind("VAL", v("su", R[0:8]), V))
+        if rd < 2:
+            act(c1("ac", rd + 1), c1("cc", 5), scale=-0.5, bias=63.625)
+            act(c1("th", rd + 1), c1("cc", 5), scale=-0.5, bias=c1("th", 3))
+        for k in range(8):
+            compare("GT", "slT", k, "sign")
+        for k in range(2):
+            ts(v("EQ", R[4 * k:4 * k + 4]), v("GT", R[4 * k:4 * k + 4]), 0.0, A.is_equal, 0.375, A.mult)
+        lowest("pA")
+        tt("first", a, v("wh", R[0:128]), A.is_lt)
+        tt("fm", a, v("wh", R[128:256]), A.is_lt)
+        mm(v("pB", R[0:256]), ("I32", "CD"), sp=False)
+        mm(b, ("pds", "RS"), st=False, sp=False)
+        mm(v("pB", R[128:256]), ("TGE", "first"), st=False)
+        mm(c, ("ONE", "C288"), ("I32", "pT"), ("I32", "pT"), ("NG", "first"), sp=False)
+        for k in range(8):
+            mm(v("pC", R[16 * k:16 * k + 16]), (v("GT", k), v("first", R[16 * k:16 * k + 16])), st=False, sp=k == 7)
+        offsets("oS", "pB", "fm", "sm", "pD")
+        ts("ntc", v("pC", R[0:128:16]), -0.03125, A.mult, 0.875 + 1 / 64.0, A.add)
+        ts("tc", v("pC", R[0:128:16]), 0.03125, A.mult, -0.875, A.add)
+        ts("ti", c, 2.0, A.add)
+        ts("tr", "ti", 30, A.bitwise_and)
+        for k in range(8):
+            if k < SCR:
+                ts(v("SC", R[k, 0:257]), v("IOC", R[0:257]), c1("tc", k), A.is_ge, 2.0, A.mult)
+            else:
+                act(v("SC", R[k, 0:257]), v("IOC", R[0:257]), F.Sign, bias=c1("ntc", k))
+        tt(v("A1", R[:, 112:128]), "tr", "r2", A.is_le)
+        ts(v("A0", R[:, 112:128]), v("A1", R[:, 112:128]), -1.0, A.mult, 1.0, A.add)
+        terms = [("I32", "C2A")]
+        for k in range(8):
+            terms += [(v("A1", R[k, 112 - 16 * k:240 - 16 * k]), v("SC", R[k, 1:257])), (v("A0", R[k, 112 - 16 * k:240 - 16 * k]), v("SC", R[k, 0:256]))]
+        mm(v("pE", R[0:256]), *terms)
+        ts("oR", v("pE", R[0:256]), 0.5, A.mult)
+        if rd < 2:
+            mm(a, (v("LW", 0), "pds"), ("ID", "vs"))
+            mm(v("pA", R[128:256]), ("first", "TLT"))
+            mm(v("pA", R[256:257]), ("first", c1("ONE", 0)))
+            act("tv", a)
+            act("pv", v("pA", R[128:256]), scale=c1("mv", 2), bias=c1("mv", rd))
+            if rd == 0:
+                ts(c1("mv", 1), v("pA", R[256:257]), c1("mv", 3), A.mult, c1("mv", 0), A.add)
+            rt = "RT%d" % rd
+            ts(rt, v("first", R[0:128:16]), -65536.0, A.mult, 65536.0, A.add)
+            tt(rt, rt, "slT", A.add)
+            cp(ind("POS", v("oS", R[0:8])), "pv")
+        else:
+            mm(a, ("RS", "pds"))
+            act("tv", a)
+
+    def nodes(rd):
+        xt = XT[rd]
+        for c in range(8):
+            measure(c, xt, "oN", -192.0, v("pK", R[c // 2:256:4]), "Z2", c == 7, c == 7)
+        scan("KS", "RST", v("pK", R[0:256]), 0.0, A.add, A.max)
+        cp("ki", v("KS", R[31:256:32]))
+        ts("kj", "ki", 8191, A.bitwise_and)
+        pl = v("pu", R[0:8])
+        ts(pl, "kj", -512.0, A.add)
+        win = ind(xt, pl)
+        sn, ln = "send%d" % rd, "land%d" % rd
+        tt("g1", win, "Kt", A.add)
+        tt("wv", win, "nd", A.add)
+        act("pdn", ind("VAL", pl, V))
+        act("xn192", win, bias=192.0)
+        act("pk", win)
+        tt("v1", "g1", "na", A.mult)
+        if rd < 2:
+            tt(sn, "v1", "wv", A.min)
+        else:
+            tt("vt", "v1", "wv", A.min)
+            ts(sn, "vt", -1.0, A.mult, -160.0, A.add)
+        trs, lands = [], []
+        for c, e in my.items():
+            rid, pid, _ = topo.addr(c)
+            b = T.rank_of(c)
+            lands.append(v(ln, R[16 * b:16 * b + 16]))
+            trs.append(RemoteDMATransfer(dst_ids=[DstId(rid=rid, pnc=pid)], dma_engine_mask=sum(1 << x for x in e), remote_sem=T.sem["arr%d" % rd],
+                                         src=v(sn, R[16 * b:16 * b + 16])["ap"], dst=v(ln, R[16 * rank:16 * rank + 16])["ap"]))
+        op("G", lambda q: q.remote_dma_fused(trs, local_sem=T.sem.sent), lands, [v(sn)], 0.5, "arr%d" % rd, arrive, 3.5, True)
+        act(v(ln, R[16 * rank:16 * rank + 16]), v(sn, R[16 * rank:16 * rank + 16]))
+
+    def near(rd):
+        spread("pdn", "slN")
+        mm(v("pK", R[256:384]), ("ONE", "NO1"), ("HP", "NO1"), ("ID", "c2"), ("ID", "xn192"))
+        ts("vn", v("pK", R[256:384]), 0.0, A.max, 63.0, A.min)
+        if rd < 2:
+            mm(v("pK", R[384:512]), ("I32", "pk"), ("NI", "xn192"), ("ID", "vn"))
+            act("nv", v("pK", R[384:512]), bias=192.0)
+        for k in range(8):
+            compare("EQ" if k < NGR else "GT", "slN", k, "eq" if k < NGR else "sign")
+        if NGR < 8:
+            ts(v("EQ", R[NGR:8]), v("GT", R[NGR:8]), 0.0, A.is_equal, 0.375, A.mult)
+        lowest("pD")
+        a, b = v("pE", R[0:128]), v("pE", R[128:256])
+        mm(v("pE", R[0:256]), ("I32", "CN"), sp=False)
+        mm(b, ("pdn", "RS"), st=False, sp=False)
+        mm(a, ("pk", "S0"), ("xn192", "NS0"), st=False)
+        tt("fn", v("pD", R[0:128]), v("wh", R[128:256]), A.is_lt)
+        offsets("oT", "pE", "fn", "sn", "pD", 2 if rd < 2 else 1)
+        if rd < 2:
+            cp(ind(XT[rd], v("oT", R[8:16])), "nv")
+        cp(ind("X", v("oT", R[0:8])), "vn")
+        cp(ind("X", v("oS", R[0:8])), "vs")
+
+    for t in range(8):
+        b, cols = v("pS%d" % (t % 2)), R[512 * t:512 * t + 512]
+        if t >= 8 - PACK_S:
+            mm(b, (v("LW", t), "VB"), ("ID", v("X", cols)))
+            act(v("XP", cols), b)
+        else:
+            mm(b, (v("LW", t), "VB"))
+            tt(v("XP", cols), b, v("X", cols), A.add)
+    reorder("XP", "XA", "Wu", FIRST_S)
+    for rd in range(3):
+        cands(rd)
+        places(rd)
+        if rd == 2:
+            dma("Y", v("seg"), v("XA", R[0:V], p=R[0:128:16]), 2.5)
+            act("sega", "seg", bias=192.0)
+            tt("segf", "seg", "sega", A.subtract)
+            act("Wf", "segf", scale=16384.0, bias=192.0 * 16384)
+            dma("Y", v("XB", R[0:V], p=R[0:128:16]), v("Wf"), 2.5)
+        match(rd)
+        nodes(rd)
+        near(rd)
+        if rd < 2:
+            reorder(XT[rd], XT[rd + 1], "oR", MOVE_S)
+            cp(ind(XT[rd + 1], v("oS", R[8:16])), "tv")
+    dma("Y", T.yx[:, 0:2048], v("X", R[0:2048]), 5.0)
+    dma("S", T.yx[:, 2048:V], v("X", R[2048:V]), 6.0)
+    dma("Y", T.yz[:], v("land2"), 2.0)
+    reorder("XB", "XP", "oR", LAST_S)
+    cp(ind("XP", v("oS", R[8:16])), "tv")
+    dma("S", T.yt[:], v("XP", R[0:V], p=R[0:128:16]), 2.5)
+    emit(g, T, arrange(ops))
+    g.wait_ge(T.sem.sent, 3 * sum(len(e) for e in my.values()))

@@ -23,47 +23,58 @@ def _group(name, dtype, width, names):
 
 
 _decl(bf, [W], "X")
-_decl(f32, [W], "XP XA XB POS")
+_decl(f32, [W], "XA XB POS")
 _decl(f32, [V], "VAL")
-_decl(bf, [V], "D")
-_decl(bf, [32, 128], "AB")
+_decl(bf, [V], "FR D")
+_decl(bf, [32, 4, 2, 16], "AB")
+_decl(bf, [8, 4, 16], "RP4")
 _decl(bf, [512], "REP")
 _decl(bf, [128], "z0 land0 land1 land2 send0 send1 send2 xs")
-_decl(u16, [32], "oZ")
-_group("gb", bf, 128, "zt pd pds pdn ad sg c2 v160 vs xn192 xn0 vt vn first fm fn "
-                      "M16 BO ID NI HI I512 ONE HP NO1 NG C288 NM WBp WBn RS RP NS0 TGE TLT MA MB MC")
-_decl(bf, [8, 128], "LW SELG EQ GT")
-_group("gc", bf, 256, "RUF RX wh sega")
-_decl(bf, [768], "TW TQ")
-_decl(bf, [512], "VB")
-_decl(bf, [144], "Z1 Z2")
+_group("gb", bf, 128, "H1 pd npd ad sg c2 vs xn r2 vn fs fr nfr mt first nfm "
+                      "ID NI HI NHI I64 N64 IX IT NB HP NO1 BO RS IA IB ZE C2K CK CF CP CH C19 TA MA")
+_decl(bf, [8, 128], "SELG EQ GT GU Y")
+_group("gc", bf, 256, "RX M16 ONE DH DL")
+_decl(bf, [3, 8, 8, 4], "TW")
+_decl(bf, [3, 8, 32], "TQ")
+_decl(bf, [3, 32], "KW KQ")
+_decl(bf, [128], "TRI")
+_decl(bf, [512], "sega")
+_decl(f32, [128], "nv")
+_group("gz", bf, 144, "Z1 Z1n Z2 Z2b Z2p")
 _decl(bf, [8, 240], "A0 A1")
 _decl(bf, [8, 264], "SC")
 _decl(bf, [264], "IOC")
-_decl(bf, [8], "WQ")
-_group("gh", f16, 128, "um Pm Um Fm I239")
-_group("gf", f32, 128, "I32 CU1 CU2 C2K CT PRD KAP uu ku Kt nd na g1 wv v1 pk pT tv nv pv S0 DM tmp tm2")
-_group("gg", f32, 256, "CD CN C2A sm sn RST RSC KA KS seg segf Wf")
+_group("gq", bf, 8, "WQ QA QB")
+_group("gh", f16, 128, "um Pm MB")
+_group("gk", f16, 256, "UF CU")
+_group("gf", f32, 128, "I32 CT PRD KAP uu pT S0 tmp rr ww PV0 PV1")
+_group("gg", f32, 256, "sn RST RSC KA KS Wf TF DMP")
+_decl(f32, [512], "seg")
 _decl(f32, [8, 16], "PA PB")
-_decl(f32, [128], "CKC")
-_decl(f32, [8, 32], "M Mt")
-_decl(f32, [64], "IO CM")
-_group("ge", f32, 8, "col LC sW slT slN RT0 RT1 tc ntc Q32 thq wq cc ac th mv")
-_group("gi", i32, 128, "mi q0 sum ti tr r2")
+_decl(i32, [8, 32], "M")
+_decl(i32, [8, 32], "Mt")
+_group("ge", f32, 8, "col sW osf plf RT0 RT1 tc ntc Q32 thq cc ac th dc")
+_group("gi", i32, 128, "mi q0 sum ti tr r1")
 _decl(i32, [8, 16], "h")
 _decl(i32, [2, 128], "L")
+_decl(i32, [256], "TN")
 _group("gj", i32, 8, "thr thb kapi ki kj")
-_decl(u16, [256], "Wu oN oR")
+_decl(u16, [256], "Wu Wn oR")
+_decl(u16, [264], "oN")
 _decl(u16, [128], "oC")
 _decl(u16, [16], "oS oT su pu")
 _decl(f32, [512], "pA pB pC pD pE pK pS0 pS1", "psum")
-SEMAPHORES = ["sV", "sS", "sP", "sG", "sent", "arr0", "arr1", "arr2"] + ["d%d" % k for k in range(16)]
-LOADS, TURNS, SHAKE = 7, 1500, 5.0
-STEP_S, STEP_V, STEP_P, HALF = 1, 1, 2, 1
-SCR, NGR = 0, 8
-CY, PE, GA, SCA, WAKE = 1.04e-3, 0.52e-3, 1.56, 3.5, 0.1
+SEMAPHORES = ["sV", "sS", "sP", "sG", "sent", "arr0", "arr1", "arr2"] + ["d%d" % k for k in range(20)]
+LOADS, TURNS, SHAKE = 8, 900, 5.0
+CY, PE, GA, SCA, WAKE = 1.04e-3, 0.52e-3, 1.56, 3.8, 0.1
+MAGIC = 12582912.0
+STEP_S, STEP_V, HALF = 1, 1, 1
+SCR = 2
 SGR = 4
-PACK_S, FIRST_S, MOVE_S, LAST_S = 1, 6, 12, 12
+PLACE_V = 0
+MOVE_S, LAST_S = 14, 12
+CANDS, NODES = ("BBBB", "BBBB", "BBBB"), ("CACAAAAA", "CACAAAAA", "CACAAAAA")
+REPC, REPN = "VVVV", "VVVV"
 
 
 def masks(topo, src, cores):
@@ -89,26 +100,26 @@ def depend(ops):
     acc, last, out = {}, {}, []
     for n, o in enumerate(ops):
         hard, soft = set(), set()
-        for name, lo, hi in o["r"]:
-            for m, l2, h2, wr in acc.get(name, []):
-                if wr and l2 <= hi and lo <= h2:
+        for name, cols in o["r"]:
+            for m, had, wr in acc.get(name, []):
+                if wr and had & cols:
                     hard.add(m)
-        for name, lo, hi in o["w"]:
+        for name, cols in o["w"]:
             keep = []
-            for m, l2, h2, wr in acc.get(name, []):
-                if l2 <= hi and lo <= h2:
+            for m, had, wr in acc.get(name, []):
+                if had & cols:
                     hard.add(m)
-                if not (lo <= l2 and h2 <= hi):
-                    keep.append((m, l2, h2, wr))
+                if had & ~cols:
+                    keep.append((m, had, wr))
             acc[name] = keep
         for bank in o["x"]:
             if bank in last:
                 (soft if ops[last[bank]]["e"] == o["e"] else hard).add(last[bank])
             last[bank] = n
-        for name, lo, hi in o["r"]:
-            acc.setdefault(name, []).append((n, lo, hi, False))
-        for name, lo, hi in o["w"]:
-            acc[name].append((n, lo, hi, True))
+        for name, cols in o["r"]:
+            acc.setdefault(name, []).append((n, cols, False))
+        for name, cols in o["w"]:
+            acc[name].append((n, cols, True))
         hard.discard(n)
         soft.discard(n)
         out.append((hard, soft - hard))
@@ -216,7 +227,7 @@ def rank_program(g, core, T, topo):
     rank = T.rank_of(core)
     if rank is None:
         return
-    ops, ndma, tag = [], [0], [None]
+    ops, ndma, tag, turn = [], [0], [None], [0]
 
     def v(name, *idx, p=slice(None)):
         shape, dtype, where = SHAPE[name]
@@ -224,7 +235,9 @@ def rank_program(g, core, T, topo):
             idx = idx[0]
         at = np.arange(int(np.prod(shape))).reshape(shape)[idx]
         ap = T[GROUP[name][0]][(p, GROUP[name][1]) + (idx or (slice(None),))] if name in GROUP else T[name][(p,) + idx]
-        span = (name, int(np.min(at)), int(np.max(at)))
+        used = np.zeros(int(np.prod(shape)), np.uint8)
+        used[np.ravel(at)] = 1
+        span = (name, int.from_bytes(bytes(np.packbits(used)), "big"))
         return {"ap": ap, "n": int(np.size(at)), "k": [span], "two": dtype in (bf, f16, u16), "ps": where == "psum", "f32": dtype == f32, "ind": False, "off": []}
 
     def c1(name, k):
@@ -292,6 +305,12 @@ def rank_program(g, core, T, topo):
             kw["accum_out"] = acc["ap"]
         op("S", lambda q: q.activation(out["ap"], a["ap"], fn, **kw), [out] + ([acc] if acc else []), [a] + list(k.values()), cost("S", out, a, 1))
 
+    def shift(e, out, a, c):
+        if e == "S":
+            act(out, a, bias=c)
+        else:
+            ts(out, a, c, A.add)
+
     def mm(out, *terms, st=True, sp=True):
         for j, (l, rr) in enumerate(terms):
             l, rr = u(l), u(rr)
@@ -308,144 +327,181 @@ def rank_program(g, core, T, topo):
         op("G", lambda q: q.affine_select(out["ap"], a["ap"], pat, o, fill, base, cm), [out], [a], 0.17 + 2 * out["n"] * CY)
 
     col = [c1("col", k) for k in range(8)]
-    Mc = [c1("M16", k) for k in range(4)]
+    M16, ONE = v("M16", R[0:128]), v("ONE", R[0:128])
     Q = v("BO", R[0:128:16])
 
-    dma("Y", v("L", 0), T.ts[0:8:2, :], 2.3)
-    dma("S", v("L", 1), T.ts[1:8:2, :], 2.6)
-    dma("Y", v("z0"), T.zq[:], 2.7)
-    dma("S", c1("kapi", 0), T.kap[:], 2.7)
+    dma("Y", v("TN"), T.ts[:], 2.2)
+    dma("S", v("L", 0), T.ts[0:8:2, :], 2.4)
+    dma("Y", v("L", 1), T.ts[1:8:2, :], 2.6)
+    dma("S", v("z0"), T.zq[:], 2.7)
+    dma("Y", c1("kapi", 0), T.kap[:], 2.7)
     dma("S", v("thr", p=R[0:1]), T.th[:], 2.7)
-    dma("Y", v("X", R[0:2048]), T.xr[:, 0:2048], 5.0)
-    dma("Y", v("X", R[2048:V]), T.xr[:, 2048:V], 7.5)
+    dma("Y", v("X", R[0:2048]), T.xr[:, 0:2048], 4.5)
+    dma("Y", v("X", R[2048:V]), T.xr[:, 2048:V], 6.5)
 
-    iota("mi", [[0, 8], [-1, 16]], 128, 1)
-    iota("IO", [[1, 64]], 0)
-    for n, c in (("ONE", 1.0), ("CT", 0.0), ("HP", 0.5)):
+    cp("Wn", "TN")
+    for t in range(8):
+        off = ind("POS", v("Wn", R[32 * t:32 * t + 32]), V)
+        tag[0] = "place"
+        if t < 8 - PLACE_V:
+            iota(v("VAL", R[512 * t:512 * t + 512]), [[1, 32], [256, 16]], 64 + 32 * t)
+            act(off, v("VAL", R[512 * t:512 * t + 512]), F.Silu)
+        else:
+            ts(off, v("VAL", R[0:512]), 1.0, A.mult, 32.0 * t, A.add)
+        tag[0] = None
+
+    ms("ONE", 1.0)
+    for n, c in (("HP", 0.5), ("NO1", -1.0), ("CT", 0.0), ("C2K", 2048.0)):
         ms(n, c)
-    for n, c in (("NO1", -1), ("CU1", -2048), ("C2K", 2048), ("C288", 288), ("CU2", -12448), ("Z1", 0), ("Z2", 0), ("tm2", 0)):
-        iota(n, [[0, v(n)["n"]]], c)
-    for n in ("X", "XA", "XB", "XP", "POS"):
-        iota(v(n, R[V:W]), [[0, W - V]], 0)
-    ms(c1("ac", 0), -0.375)
-    sel("tmp", "ONE", [[-16, 8], [0, 16]], A.is_ge, 0, 1)
+    ms(v("FR", R[0:256]), 0.0)
+    for k in (256, 512, 1024):
+        act(v("FR", R[k:2 * k]), v("FR", R[0:k]))
+    for k in range(2, 4):
+        ms(v("FR", R[1024 * k:1024 * k + 1024]), 0.0)
+    ms("ZE", 0.0)
+    iota("mi", [[0, 8], [-1, 16]], 128, 1)
+    sel("tmp", ONE, [[-16, 8], [0, 16]], A.is_ge, 0, 1)
     sel("BO", "tmp", [[16, 8], [0, 16]], A.is_ge, 15, -1)
+    sel("ID", ONE, [[-1, 128]], A.is_equal, 0, 1)
     iota(v("CT", R[0:16:2]), [[1, 8]], 1)
     iota(v("CT", R[1:14:2]), [[-1, 7]], 7)
-    sel("ID", "ONE", [[-1, 128]], A.is_equal, 0, 1)
+    iota(c1("CT", 15), [[0, 1]], 1)
+    iota(v("CT", R[16:18]), [[0, 2]], 1)
+    iota(c1("CT", 33), [[0, 1]], 1)
+    iota(v("CT", R[48:64]), [[1, 16]], 0)
     ts("q0", "mi", 15, A.bitwise_and)
-    ts("M16", "q0", 0.0, A.is_equal)
-    ts(v("VAL", R[0:64]), "IO", Mc[1], A.mult, 128.0, A.add)
-    ts("CM", "IO", Mc[0], A.mult)
-    for k in (1, 2, 4):
-        ts(v("VAL", R[64 * k:128 * k]), v("VAL", R[0:64 * k]), c1("CM", k), A.add)
-    for t in range(1, 8):
-        ts(v("VAL", R[512 * t:512 * t + 512]), v("VAL", R[0:512]), c1("CM", 8 * t), A.add)
-    for g0 in range(2):
-        cp(v("M", R[:, 16 * g0:16 * g0 + 16]), v("L", g0))
-    for c in range(8):
-        a, b = v("Mt", c), v("M", c)
-        op("V", lambda q, a=a, b=b: q.transpose(a["ap"], b["ap"]), [a], [b], 64 * CY)
-        cp(v("Wu", R[c:256:8]), a)
-    for t in range(0, 16, STEP_P):
-        act(ind("POS", v("Wu", R[16 * t:16 * (t + STEP_P)]), V), v("VAL", R[256 * t:256 * (t + STEP_P)]), F.Silu)
-    for at, c in ((15, 1.0), (16, 64.0), (19, -66.0), (32, 2.0 ** -8), (33, 2.0 ** -14), (35, -65 * 2.0 ** -14), (48, 16384.0), (64, 64.0), (67, -82.0),
-                  (68, -1 / 128.0), (83, -16.0), (84, 1 / 128.0), (99, 12.0), (100, -15 / 4096.0)):
-        if c == int(c):
-            iota(c1("CT", at), [[0, 1]], int(c))
-        else:
-            ms(c1("CT", at), c)
-    iota(v("CT", R[17:19]), [[0, 2]], 1)
-    iota(v("CT", R[65:67]), [[0, 2]], 1)
-    iota(v("CT", R[113:128]), [[0, 15]], 128)
-    iota(c1("CT", 112), [[0, 1]], 192)
-    tt("PRD", "CT", "M16", A.mult)
-    for k in range(8):
+    for k in range(2):
+        ts(v("M16", R[128 * k:128 * k + 128]), "q0", 0.0, A.is_equal)
+    tt(v("PRD", R[0:64]), v("CT", R[0:64]), v("M16", R[0:64]), A.mult)
+    for k in range(4):
         red(col[k], v("PRD", R[16 * k:16 * k + 16]))
+    for n in ("X", "XA", "XB", "POS"):
+        iota(v(n, R[V:W]), [[0, W - V]], 0)
+    ms(c1("ac", 0), -0.375)
     cp("I32", "ID")
     cp(c1("cc", 0), c1("kapi", 0))
-    ts("tmp", "M16", c1("cc", 0), A.mult)
+    ts("tmp", M16, c1("cc", 0), A.mult)
     cp("S0", "BO")
     mm(v("pD", R[0:128]), ("S0", "tmp"))
     cp("KAP", v("pD", R[0:128]))
-    iota("CKC", [[16384, 2], [0, 8], [2048, 8]], -16711680)
     a, b = v("thb"), v("thr", p=R[0:1])
     op("G", lambda q, a=a, b=b: q.partition_broadcast(a["ap"], b["ap"], 128), [a], [b], 0.2)
-    ts("LC", v("IO", R[0:8]), Mc[3], A.mult, 2.0 ** -12, A.mult)
-    ts("LC", "LC", col[2], A.add)
-    cp("VB", v("VAL", R[0:512]))
-    ts(v("Z1", R[15:128:16]), Q, 32768.0, A.mult)
-    ts(v("Z2", R[15:128:16]), Q, -8192.0, A.mult)
-    for t in range(8):
-        ts(v("LW", t), "BO", c1("LC", t), A.mult)
-    for n, c in (("NI", -1.0), ("HI", 0.5), ("I512", 512.0), ("I239", 239.75)):
-        ts(n, "ID", c, A.mult)
-    for n, c in (("MA", -1664.0), ("MB", 2048.0), ("MC", 2560.0)):
-        ts(n, "M16", c, A.mult)
-    ts("NM", "M16", 4.0, A.mult, -4.0, A.add)
-    for n, k, c in (("WBp", 0, 1.0), ("WBn", 0, -1.0), ("RS", 1, 1.0), ("RP", 4, 1.0), ("S0", 3, 1.0), ("NS0", 3, -1.0), (v("RUF", R[0:128]), 5, 1.0),
-                    (v("RUF", R[128:256]), 6, 1.0), (v("RX", R[0:128]), 0, 1.0), (v("RX", R[128:256]), 0, 0.0625)):
-        ts(n, "BO", col[k], A.mult, c, A.mult)
-    ts("wq", Q, col[1], A.mult)
-    cp("WQ", "wq")
-    cp("Q32", Q)
+    both = "".join(CANDS), "".join(NODES)
+    for n, c, need in (("Z1", 32768.0, True), ("Z1n", -32768.0, "B" in both[0]), ("Z2", -8192.0, True), ("Z2b", -16384.0, "B" in both[1]), ("Z2p", 8192.0, "B" in both[1])):
+        if need:
+            iota(n, [[0, 144]], 0)
+            ts(v(n, R[15:128:16]), Q, c, A.mult)
+    for n, c in (("NI", -1.0), ("HI", 0.5), ("NHI", -0.5), ("I64", 64.0), ("N64", -64.0), ("IX", 32.0), ("IT", 1 / 64.0), ("NB", -2.0 ** 23),
+                 ("IA", 1032.0 * 8192), ("IB", -2040.0 * 8192)):
+        sel(n, "ZE", [[-1, 128]], A.not_equal, 0, 1, c)
+    for n, c in (("MA", -1664.0), ("MB", 2047.0)):
+        ts(n, M16, c, A.mult)
+    WB = v("RX", R[0:128])
+    for n, c in ((WB, 1.0), (v("RX", R[128:256]), 0.0625)):
+        ts(n, "BO", col[0], A.mult, c, A.mult)
+    sel("RS", "BO", [[16, 8], [0, 16]], A.is_ge, 1, -1)
+    for n, c in (("CK", -504 * 32768), ("CP", -2112), ("C19", 2 ** 19), (v("CU", R[0:128]), -2047), (v("CU", R[128:256]), 1536),
+                 ("PV0", V + 64), ("PV1", V + 192)):
+        iota(n, [[1 if n in ("PV0", "PV1") else 0, 128]], c)
+    for n, c in (("CF", -15 / 32.0), ("CH", 63.75)):
+        ms(n, c)
+    ts("thq", Q, col[1], A.mult, 512.0, A.mult)
+    cp("WQ", "thq")
     for k in range(8):
-        ts(v("SELG", k), "ONE", c1("wq", k), A.mult)
-    for n, pk_, pq in (("TW", lambda s: [[4 * s, 8], [0, 8], [s, 4]], lambda s: [[0, 24], [s, 8], [0, 4]]),
-                       ("TQ", lambda s: [[0, 8], [s, 8], [8 * s, 4]], lambda s: [[0, 3], [s, 8], [0, 32]])):
-        for j, (s, base) in enumerate(((0, 1), (-1, 0), (16, 0))):
-            iota(v(n, R[256 * j:256 * j + 256]), pk_(s), base)
-        sel(n, n, pq(-16), A.is_ge, 0, 1)
-        sel(n, n, pq(16), A.is_ge, 15, -1)
-    iota("RST", [[0, 256]], 0)
-    sel("RSC", "RST", [[0, 16], [1, 16]], A.not_equal, 0, 0, 1e9)
-    sel("RST", "RST", [[0, 8], [1, 32]], A.not_equal, 0, 0, -1e9)
-    iota("r2", [[0, 8], [2, 16]], 0)
+        ts(v("SELG", k), ONE, c1("thq", k), A.mult)
+    iota(c1("cc", 2), [[0, 1]], 0, 1)
+    ts("Q32", Q, 16384.0, A.mult)
+    ts("QA", Q, 4096.0, A.mult)
+    ts("QB", Q, c1("cc", 2), A.mult)
+    iota(v("dc", R[0:2]), [[128, 2]], V + 64, 1)
+    ts(v("dc", R[2:4]), v("dc", R[0:2]), 512.0, A.mult)
+    ts(c1("dc", 4), c1("cc", 2), 2.0 ** -14, A.mult, 0.25, A.add)
+    ts("DMP", "M16", c1("dc", 4), A.mult)
+    ts(c1("cc", 7), c1("cc", 2), 16.0 * SCR, A.is_ge, 64.0, A.mult)
+    tt(c1("cc", 6), c1("cc", 7), col[3], A.add)
+    for j, (s, base) in enumerate(((0, 1), (-1, 0), (16, 0))):
+        iota(v("KW", j), [[s, 32]], base)
+        iota(v("KQ", j), [[s, 4], [4 * s, 2], [8 * s, 4]], base)
+    for k in range(8):
+        ts(v("TW", R[:, :, k]), "KW", c1("BO", 16 * k), A.mult)
+        ts(v("TQ", R[:, k]), "KQ", c1("BO", 16 * k), A.mult)
+    for n, c, step, start in (("RST", 0, 32, -1e9), ("RSC", -2048, 16, 1e9)):
+        iota(n, [[0, 256]], c)
+        ms(v(n, R[0:256:step]), start)
+    iota("r1", [[0, 8], [1, 16]], 0)
     iota("IOC", [[1, 264]], -1)
-    iota("CD", [[4096, 2], [0, 128]], -4096, -1)
-    iota(v("CN", R[0:128]), [[0, 128]], 192 * 16384 - 4096, -1)
-    iota(v("CN", R[128:256]), [[0, 128]], -4096, -1)
-    iota("C2A", [[32, 256]], 0)
-    sel("TGE", "NO1", [[-1, 128]], A.is_ge, 0, 1)
-    sel("TLT", "ONE", [[1, 128]], A.is_gt, 0, -1)
-    sel("NG", "NO1", [[-1, 128]], A.not_equal, 0, 1, -32768.0)
-    iota(c1("cc", 2), [[0, 1]], 4096, 1)
-    for n in ("A0", "A1"):
-        for k in range(4):
-            iota(v(n, R[2 * k:2 * k + 2]), [[0, 480]], 0)
-    tt("thq", "thb", "Q32", A.mult)
-    red(c1("cc", 1), "thq")
+    iota("TA", [[0, 128]], -256)
+    sel("TA", "TA", [[-1, 128]], A.is_gt, 0, 1)
+    sel("TRI", ONE, [[1, 128]], A.is_gt, 0, -1)
+    for k in range(4):
+        iota(v("A0", R[2 * k:2 * k + 2]), [[0, 480]], 0)
+    dma("Y", v("A1"), v("A0"), 2.5)
+    ts("osf", Q, 1.0, A.mult)
+    tt("plf", "thb", "osf", A.mult)
+    red(c1("cc", 1), "plf")
     ts(c1("th", 0), c1("cc", 1), 0.5, A.add)
     ts(c1("th", 3), c1("cc", 1), 64.5, A.add)
-    ts("DM", "M16", c1("cc", 2), A.mult)
-    scan("PRD", "HP", "tm2", 2.0 ** 64, A.mult, A.add)
-    tt("tmp", "PRD", "I32", A.mult)
-    red(c1("cc", 3), "tmp")
-    tt(v("uu", R[0:16]), v("M16", R[0:16]), v("IO", R[0:16]), A.mult)
-    red(c1("cc", 6), v("uu", R[0:16]))
-    iota(v("ku", R[0:32]), [[16, 8], [0, 4]], 0)
-    ts("oZ", v("ku", R[0:32]), c1("cc", 6), A.add)
-    ts(c1("cc", 4), c1("cc", 6), 2.0, A.mult)
-    ts(c1("cc", 7), c1("cc", 2), 4096.0 + 16 * SCR, A.is_ge, 128.0, A.mult)
-    ts("C2A", "C2A", c1("cc", 4), A.add, c1("cc", 7), A.add)
-    cp(c1("mv", 0), col[7])
-    cp(c1("mv", 2), Mc[1])
-    cp(c1("mv", 3), Mc[2])
+
+    for g0 in range(2):
+        cp(v("M", R[:, 16 * g0:16 * g0 + 16]), v("L", g0))
+    a, b = v("Mt"), v("M")
+    op("V", lambda q, a=a, b=b: q.transpose(a["ap"], b["ap"]), [a], [b], 256 * CY)
+    for c in range(8):
+        cp(v("Wu", R[c:256:8]), v("Mt", c))
+    ts("TF", "TN", 2.0 ** -14, A.mult)
+    ts("DH", "TN", 2.0 ** -14, A.mult)
+    mm(v("pE", R[0:256]), ("I32", "TF"), ("NI", "DH"))
+    cp("DL", v("pE", R[0:256]))
+    dma("Y", v("FR", p=R[0:128:16]), v("DH"), 2.0)
+    dma("Y", v("FR", p=R[1:128:16]), v("DL"), 2.0)
+    tag[0] = "first"
+    for t in range(8):
+        cols = R[512 * t:512 * t + 512]
+        tt(v("XA", cols), ind("X", v("Wu", R[32 * t:32 * t + 32]), V), v("FR", cols), A.add)
+    tag[0] = None
 
     my = masks(topo, core, T.cores)
     arrive = sum(len(masks(topo, c, T.cores)[core]) for c in T.cores if c != core)
     XT = ["XA", "XB", "XA"]
+    blk = lambda b: R[16 * b:16 * b + 16]
 
-    def measure(c, win, off, bias, key, zz, last, end):
-        tag[0] = "measure"
-        for a, b in ((0, 5), (5, 8)) if HALF and end else ((0, 8),):
-            d = v("D", R[512 * c + 64 * a:512 * c + 64 * b])
-            tt(d, ind(win, v(off, R[32 * c + 4 * a:32 * c + 4 * b])), v("REP", R[64 * a:64 * b]), A.add)
-            act(v("AB", R[8 * (c // 2) + a:8 * (c // 2) + b, 64 * (c % 2):64 * (c % 2) + 64]), d, F.Abs, bias=bias)
-        tag[0] = None
-        if c % 2:
-            b = c // 2
-            mm(key, *[(v(zz, R[15 - r:143 - r]), v("AB", R[8 * b:8 * b + 8, r:128:16])) for r in range(16)], st=False, sp=last)
+    def piece(c, n):
+        return v("pK", R[n // 2 * (c % 2) + c // 2:32 * n:n])
+
+    def repeat(engines, src, c):
+        for k in range(4):
+            shift(engines[k], v("RP4", R[:, k]), src, c)
+        cp("REP", "RP4")
+
+    def measure(c, hows, win, off, bias, zz):
+        how = hows[c]
+        for a, b in ((0, 5), (5, 8)) if HALF and c == len(hows) - 1 and how == "A" else ((0, 8),):
+            d, size = v("D", R[512 * c + 64 * a:512 * c + 64 * b]), v("AB", R[8 * (c // 2) + a:8 * (c // 2) + b, :, c % 2])
+            src = ind(win, v(off, R[32 * c + 4 * a:32 * c + 4 * b]))
+            if how == "C":
+                bank = v(("pA", "pB")[turn[0] % 2], R[64 * a:64 * b])
+                turn[0] += 1
+                act(d, src, bias=bias)
+                mm(bank, ("NI", v("REP", R[64 * a:64 * b])), ("ID", d))
+                act(size, bank, F.Abs, bias=-2 * bias)
+                continue
+            tt(d, src, v("REP", R[64 * a:64 * b]), A.subtract)
+            if how == "A":
+                act(size, d, F.Abs, bias=-bias)
+            elif bias:
+                ts(size, d, -bias, A.add, 0.0, A.max)
+            else:
+                ts(size, d, 0.0, A.max, 2.0, A.mult)
+        b, n = c // 2, len(hows)
+
+        def sums(out, z, rhs, stop):
+            mm(out, *[(v(z, R[15 - r:143 - r]), rhs(r)) for r in range(16)], st=False, sp=stop)
+        if how == "B":
+            sums(piece(c, n), zz[2], lambda r: v("D", R[512 * c + r:512 * c + 512:16]), False)
+        if (hows[2 * b] == "B") != (hows[2 * b + 1] == "B"):
+            sums(piece(c, n), zz[how == "B"], lambda r: v("AB", R[8 * b:8 * b + 8, :, c % 2, r]), c == n - 1)
+        elif c % 2:
+            sums(v("pK", R[b:32 * n:n // 2]), zz[how == "B"], lambda r: v("AB", R[8 * b:8 * b + 8, :, :, r]), c == n - 1)
 
     def reorder(src, dst, lst, on_s):
         t = 0
@@ -457,249 +513,232 @@ def rank_program(g, core, T, topo):
             tag[0] = None
             t += k
 
-    def cands(rd):
-        zb = "z0" if rd == 0 else "land%d" % (rd - 1)
-        sc, bi = (1.0, 0.0) if rd == 0 else (-1.0, -160.0)
+    def cands(rd, zb):
         ut = v("pA", R[0:128])
-        mm(ut, ("I32", "CU2" if rd else "CU1"), (zb, "WBn" if rd else "WBp"))
-        tt("um", ut, "M16", A.mult)
+        mm(ut, ("NI", "C2K"), (zb, WB))
+        tt("um", ut, M16, A.mult)
         for b in ("pB", "pC"):
-            mm(v(b, R[0:128]), ("I32", "C2K"), ("um", "BO"))
-        keys = [v("pA", R[128:192]), v("pK", R[0:64])]
-        for b in range(2):
-            mm(keys[b], ("I32", v("CKC", R[64 * b:64 * b + 64])), sp=False)
-        act("REP", ind(zb, v("oZ"), 128), scale=-sc, bias=-bi)
-        act("zt", zb, scale=sc, bias=bi)
+            mm(v(b, R[0:128]), ("ID", "C2K"), ("um", "BO"))
+        keys = v("pK", R[0:128])
+        mm(keys, ("ID", "CK"), sp=False)
+        repeat(REPC, zb, 0.0)
         act("uu", v("pB", R[0:128]), F.Square)
         tt(v("pC", R[128:256]), v("pC", R[0:128]), "KAP", A.mult)
         ts("q0", "uu", 0.03125, A.mult, c1("ac", rd), A.add)
         tt("sum", v("pC", R[128:256]), "q0", A.add)
         ts("h", "sum", V - 1, A.bitwise_and)
         for c in range(4):
-            cp(v("oC", R[32 * c:32 * c + 32]), v("h", R[:, 4 * c:4 * c + 4]))
-            measure(c, "X", "oC", 0.0, keys[c // 2], "Z1", True, c == 3 and rd > 0)
-        ts("PB", "h", -2048.0, A.add, 0.0, A.max)
-        ts("PA", "h", -2048.0, A.add, 0.0, A.min)
-        for b in range(2):
-            tt(v("KA", R[b:128:2]), keys[b], v("PA", R[:, 8 * b:8 * b + 8]), A.subtract)
-            tt(v("KA", R[128 + b:256:2]), keys[b], v("PB", R[:, 8 * b:8 * b + 8]), A.add)
+            cp(v("oC", R[32 * c:32 * c + 32]), v("h", R[:, 2 * (c % 2) + c // 2:16:4]))
+            measure(c, CANDS[rd], "X", "oC", 0.0, ("Z1", "Z1", "Z1n"))
+        ts("PB", "h", 2048.0, A.max, -2048.0, A.add)
+        ts("PA", "h", 2048.0, A.min)
+        tt(v("KA", R[0:128]), keys, "PA", A.subtract)
+        tt(v("KA", R[128:256]), keys, "PB", A.add)
         scan("KS", "RSC", "KA", 0.0, A.add, A.min)
         tt("sW", v("KS", R[143:256:16]), v("KS", R[15:128:16]), A.subtract)
-        ts(v("su", R[0:8]), "sW", 2048.0, A.add)
+        cp(v("su", R[0:8]), "sW")
 
-    def spread(digits, cols):
-        for k in range(8):
-            mm(v("pS%d" % (k // 4), R[128 * (k % 4):128 * (k % 4) + 128]), (v("SELG", k), digits))
-        mm(v("pD", R[256:264]), (digits, "WQ"))
-        act(cols, v("pD", R[256:264]))
+    def bank4(k):
+        return v("pS%d" % (k // 4), R[128 * (k % 4):128 * (k % 4) + 128])
 
-    def compare(out, cols, k, how):
-        src = v("pS%d" % (k // 4), R[128 * (k % 4):128 * (k % 4) + 128])
-        if how == "eq":
-            ts(v(out, k), src, c1(cols, k), A.is_equal, 0.375, A.mult)
-        elif how == "gt":
-            ts(v(out, k), src, c1(cols, k), A.is_gt)
-        else:
-            act(v(out, k), src, F.Sign, scale=-1.0, bias=c1(cols, k))
+    def pairs(digits, minus, tri):
+        for b in range(2):
+            for k in range(4 * b, 4 * b + 4):
+                mm(bank4(k), (tri, "TRI"), st=k % 4 == 0, sp=False)
+            for k in range(4 * b, 4 * b + 4):
+                mm(bank4(k), (v("SELG", k), digits), (minus, v("SELG", k)), st=False, sp=k % 4 == 3)
 
     def places(rd):
         sl, P = v("su", R[0:8]), v("pA", R[0:128])
         cp("xs", ind("X", sl))
-        act("pd", ind("POS", sl))
-        n1, n2, kn = v("pC", R[0:64]), v("pE", R[0:192]), v("pK", R[0:256])
-        tw = lambda j, a, b: v("TW", R[256 * j + a:256 * j + b])
-        tq = lambda j: v("TQ", R[256 * j:256 * j + 256])
+        act("H1", ind("POS", sl), scale=col[2])
+        tt("pd", ind("POS", sl), "H1", A.subtract)
+        n1, n2, n3, kn = v("pC", R[0:64]), v("pE", R[0:192]), v("pE", R[192:200]), v("pK", R[0:256])
+        tw = lambda j, a, b: v("TW", R[j, a // 32:b // 32])
+        tq = lambda j: v("TQ", j)
         mm(n1, ("MA", tw(2, 0, 64)), ("MB", tw(0, 0, 64)), sp=False)
         mm(n2, ("MA", tw(2, 64, 256)), ("MB", tw(0, 64, 256)), sp=False)
-        mm(kn, ("MA", tq(2)), ("MC", tq(0)), sp=False)
-        if rd:
-            spread("pd", "slT")
-        mm(v("pB", R[0:256]), ("xs", "RX"), ("pd", "RUF"))
-        mm(P, ("pd", "RP"), sp=rd == 0)
+        mm(n3, ("MB", Q), (M16, Q), st=False, sp=False)
+        mm(kn, ("MA", tq(2)), ("MB", tq(0)), sp=False)
+
+        mm(v("pB", R[0:256]), ("ID", "CU"), sp=False)
+        mm(v("pB", R[128:256]), ("ID", "CF"), st=False, sp=False)
+        mm(v("pB", R[0:256]), ("xs", "RX"), st=False)
+        mm(P, ("ID", "CP"), sp=False)
         if rd:
             mm(v("pA", R[16 * SGR:128]), *[("HP", v("NO1", R[16 * SGR:128]))] * rd, st=False, sp=False)
-        act("REP", ind("xs", v("oZ"), 128), scale=-1.0, bias=192.0)
-        for s in range(rd):
-            buf = ("GT", "EQ")[s]
             for k in range(8):
-                compare(buf, "RT%d" % s, k, "gt" if k < SGR else "sign")
+                mm(bank4(k), (v("SELG", k), "pd"))
+        mm(P, ("pd", "RS"), st=False, sp=rd == 0)
+        repeat(REPN, "xs", -192.0)
+        for s in range(rd):
+            buf = ("GT", "GU")[s]
+            for k in range(8):
+                if k < SGR:
+                    ts(v(buf, k), bank4(k), c1("RT%d" % s, k), A.is_gt)
+                else:
+                    act(v(buf, k), bank4(k), F.Sign, scale=-1.0, bias=c1("RT%d" % s, k))
             for k in (0, 4, 1, 5, 2, 6, 3, 7):
                 mm(v("pA", R[16 * k:16 * k + 16]), (v(buf, k), v("NO1" if k < SGR else "HP", R[0:16])), st=False, sp=s == rd - 1 and k == 7)
-        tt("Um", v("pB", R[0:128]), "M16", A.mult)
-        tt("Fm", v("pB", R[128:256]), "M16", A.mult)
-        tt("Pm", P, "M16", A.mult)
-        mm(n1, ("Um", tw(1, 0, 64)), ("Fm", tw(2, 0, 64)), ("Pm", tw(0, 0, 64)), st=False)
-        mm(n2, ("Um", tw(1, 64, 256)), ("Fm", tw(2, 64, 256)), ("Pm", tw(0, 64, 256)), st=False)
-        mm(kn, ("Um", tq(1)), ("Fm", tq(2)), ("Pm", tq(0)), st=False, sp=False)
+        tt("UF", v("pB", R[0:256]), "M16", A.mult)
+        tt("Pm", P, M16, A.mult)
+        Um, Fm = v("UF", R[0:128]), v("UF", R[128:256])
+        mm(n1, (Um, tw(1, 0, 64)), (Fm, tw(2, 0, 64)), ("Pm", tw(0, 0, 64)), st=False)
+        mm(n2, (Um, tw(1, 64, 256)), (Fm, tw(2, 64, 256)), ("Pm", tw(0, 64, 256)), st=False, sp=False)
+        mm(n3, ("Pm", Q), st=False)
+        mm(kn, (Um, tq(1)), (Fm, tq(2)), ("Pm", tq(0)), st=False, sp=False)
+        for c in range(8) if "B" in NODES[rd] else ():
+            mm(piece(c, 8), ("IB" if NODES[rd][c] == "B" else "IA", v("ONE", R[0:32])), st=False, sp=False)
         cp(v("oN", R[0:64]), n1)
-        cp(v("oN", R[64:256]), n2)
-        if rd == 0:
-            spread("pd", "slT")
+        cp(v("oN", R[64:264]), v("pE", R[0:200]))
+        act("pT", P, scale=-256.0)
 
-    def lowest(bank):
-        for k in range(8):
-            mm(v(bank, R[16 * k:16 * k + 16]), (v("EQ", k), v("wh", R[16 * k:16 * k + 16])))
-
-    def offsets(o, src, flag, buf, bank, n=2):
-        for j in range(n):
-            tt(v(buf, R[128 * j:128 * j + 128]), v(src, R[128 * j:128 * j + 128]), flag, A.mult)
-        for j in range(n):
-            mm(v(bank, R[8 * j:8 * j + 8]), ("DM", "Q32"), (v(buf, R[128 * j:128 * j + 128]), "Q32"))
-        cp(v(o, R[0:8 * n]), v(bank, R[0:8 * n]))
-
-    def match(rd):
-        a, b, c, d = (v(x, R[0:128]) for x in ("pA", "pB", "pC", "pD"))
-        act("pT", a)
-        mm(b, ("ID", "zt"), ("NI", "xs"))
-        mm(c, ("HI", "zt"), ("HI", "xs"))
-        act("ad", b, F.Abs)
-        ts("c2", b, -2.0, A.max, 2.0, A.min)
-        mm(a, ("BO", "ad"))
-        act("v160", c, bias=159.75)
-        act("sg", a, F.Sign, c1("cc", 5), scale=-1.0, bias=c1("th", rd))
-        act("vs", "v160", bias=-160.0)
-        mm(d, ("sg", "ID"))
-        mm(v("pD", R[128:256]), ("sg", "ID"), ("ID", "NM"))
-        mm(a, ("ID", "zt"), ("I239", "sg"))
-        mm(c, ("NI", "zt"), ("I512", "sg"))
-        act("wh", v("pD", R[0:256]), F.Relu, scale=c1("cc", 3))
-        act("Kt", a, F.Abs, bias=79.75)
-        act("nd", c, bias=352.0)
-        act("na", "sg", scale=0.25, bias=-0.75)
-        act("pds", ind("VAL", v("su", R[0:8]), V))
+    def match(rd, zb):
+        d0, d1, d2, d3 = (v("pD", R[128 * k:128 * k + 128]) for k in range(4))
+        mm(d0, ("ID", zb), ("NI", "xs"))
+        act("ad", d0, F.Abs)
+        ts("c2", d0, -2.0, A.max, 2.0, A.min)
+        mm(d2, ("BO", "ad"))
+        act("sg", d2, F.Sign, c1("cc", 5), scale=-1.0, bias=c1("th", rd))
         if rd < 2:
             act(c1("ac", rd + 1), c1("cc", 5), scale=-0.5, bias=63.625)
             act(c1("th", rd + 1), c1("cc", 5), scale=-0.5, bias=c1("th", 3))
+        mm(d3, ("sg", "ID"))
+        act("mt", d3, F.Relu)
+        mm(d1, ("NHI", "HP"), ("HI", zb), ("HI", "xs"))
+        ts("vs", d1, MAGIC, A.add, -MAGIC, A.add)
+        tt("fs", ind(XT[rd], v("oN", R[256:264])), "xs", A.subtract)
+        ts("npd", "pd", -1.0, A.mult)
+        pairs("pd", "npd", "ID")
+        for b in range(2):
+            ts(v("Y", R[4 * b:4 * b + 4]), v("pS%d" % b), 0.0, A.max, 256.0, A.min)
+        mm(d0, ("HI", ONE), ("sg", "NHI"), sp=False)
         for k in range(8):
-            compare("GT", "slT", k, "sign")
-        for k in range(2):
-            ts(v("EQ", R[4 * k:4 * k + 4]), v("GT", R[4 * k:4 * k + 4]), 0.0, A.is_equal, 0.375, A.mult)
-        lowest("pA")
-        tt("first", a, v("wh", R[0:128]), A.is_lt)
-        tt("fm", a, v("wh", R[128:256]), A.is_lt)
-        mm(v("pB", R[0:256]), ("I32", "CD"), sp=False)
-        mm(b, ("pds", "RS"), st=False, sp=False)
-        mm(v("pB", R[128:256]), ("TGE", "first"), st=False)
-        mm(c, ("ONE", "C288"), ("I32", "pT"), ("I32", "pT"), ("NG", "first"), sp=False)
+            mm(v("pD", R[16 * k:16 * k + 16]), (v("Y", k), v("mt", R[16 * k:16 * k + 16])), st=False, sp=k == 7)
+        ts("rr", d0, 256 * MAGIC, A.add, -256 * MAGIC, A.add)
+        tt("first", d0, "rr", A.is_equal)
+        tt("nfm", "first", M16, A.is_lt)
+        w = v("pD", R[128:136])
+        mm(w, ("nfm", "QA"), ("nfm", "QB"))
+        tt("osf", w, "sW", A.max)
+        cp(v("oS", R[0:8]), "osf")
+        if rd < 2:
+            w = v("pD", R[136:144])
+            mm(w, ("NB", v("NO1", R[0:8])), ("pd", "WQ"), ("NB", v("first", R[0:128:16])))
+            ts("RT%d" % rd, w, c1("dc", 2 + rd), A.min)
+            act(ind("POS", v("oS", R[0:8])), "PV%d" % rd, F.Silu)
+        a, b = v("pC", R[0:128]), v("pC", R[128:256])
+        mm(b, ("ID", "C19"), ("ID", "C19"), (ONE, ONE), ("TA", "first"), sp=False)
+        mm(a, ("ID", "C19"), ("I32", "pT"), ("TA", "first"), st=False, sp=False)
         for k in range(8):
-            mm(v("pC", R[16 * k:16 * k + 16]), (v("GT", k), v("first", R[16 * k:16 * k + 16])), st=False, sp=k == 7)
-        offsets("oS", "pB", "fm", "sm", "pD")
-        ts("ntc", v("pC", R[0:128:16]), -0.03125, A.mult, 0.875 + 1 / 64.0, A.add)
-        ts("tc", v("pC", R[0:128:16]), 0.03125, A.mult, -0.875, A.add)
-        ts("ti", c, 2.0, A.add)
-        ts("tr", "ti", 30, A.bitwise_and)
+            mm(v("pC", R[16 * k:16 * k + 16]), (v("Y", k), v("first", R[16 * k:16 * k + 16])), st=False, sp=k == 7)
+        tt("ww", a, "first", A.mult)
+        tt("ti", b, "ww", A.subtract)
+        if SCR < 8:
+            ts("ntc", v("ti", R[0:128:16]), -2.0 ** -12, A.mult, 1.0, A.add)
+        if SCR:
+            ts("tc", v("ti", R[0:128:16]), 2.0 ** -12, A.mult, -1.0, A.add)
+        ts("tr", "ti", 8, A.arith_shift_right, 15, A.bitwise_and)
         for k in range(8):
             if k < SCR:
                 ts(v("SC", R[k, 0:257]), v("IOC", R[0:257]), c1("tc", k), A.is_ge, 2.0, A.mult)
             else:
                 act(v("SC", R[k, 0:257]), v("IOC", R[0:257]), F.Sign, bias=c1("ntc", k))
-        tt(v("A1", R[:, 112:128]), "tr", "r2", A.is_le)
+        tt(v("A1", R[:, 112:128]), "tr", "r1", A.is_le)
         ts(v("A0", R[:, 112:128]), v("A1", R[:, 112:128]), -1.0, A.mult, 1.0, A.add)
-        terms = [("I32", "C2A")]
+        terms = [("IX", v("IOC", R[1:257]))]
         for k in range(8):
             terms += [(v("A1", R[k, 112 - 16 * k:240 - 16 * k]), v("SC", R[k, 1:257])), (v("A0", R[k, 112 - 16 * k:240 - 16 * k]), v("SC", R[k, 0:256]))]
         mm(v("pE", R[0:256]), *terms)
-        ts("oR", v("pE", R[0:256]), 0.5, A.mult)
-        if rd < 2:
-            mm(a, (v("LW", 0), "pds"), ("ID", "vs"))
-            mm(v("pA", R[128:256]), ("first", "TLT"))
-            mm(v("pA", R[256:257]), ("first", c1("ONE", 0)))
-            act("tv", a)
-            act("pv", v("pA", R[128:256]), scale=c1("mv", 2), bias=c1("mv", rd))
-            if rd == 0:
-                ts(c1("mv", 1), v("pA", R[256:257]), c1("mv", 3), A.mult, c1("mv", 0), A.add)
-            rt = "RT%d" % rd
-            ts(rt, v("first", R[0:128:16]), -65536.0, A.mult, 65536.0, A.add)
-            tt(rt, rt, "slT", A.add)
-            cp(ind("POS", v("oS", R[0:8])), "pv")
-        else:
-            mm(a, ("RS", "pds"))
-            act("tv", a)
+        ts("oR", v("pE", R[0:256]), 0.5, A.mult, c1("cc", 6), A.add)
 
-    def nodes(rd):
+    def nodes(rd, zb):
         xt = XT[rd]
         for c in range(8):
-            measure(c, xt, "oN", -192.0, v("pK", R[c // 2:256:4]), "Z2", c == 7, c == 7)
+            measure(c, NODES[rd], xt, "oN", 192.0, ("Z2", "Z2b", "Z2p"))
         scan("KS", "RST", v("pK", R[0:256]), 0.0, A.add, A.max)
-        cp("ki", v("KS", R[31:256:32]))
+        ts("ki", v("KS", R[31:256:32]), 512.0, A.add)
         ts("kj", "ki", 8191, A.bitwise_and)
         pl = v("pu", R[0:8])
         ts(pl, "kj", -512.0, A.add)
         win = ind(xt, pl)
         sn, ln = "send%d" % rd, "land%d" % rd
-        tt("g1", win, "Kt", A.add)
-        tt("wv", win, "nd", A.add)
-        act("pdn", ind("VAL", pl, V))
-        act("xn192", win, bias=192.0)
-        act("pk", win)
-        tt("v1", "g1", "na", A.mult)
-        if rd < 2:
-            tt(sn, "v1", "wv", A.min)
-        else:
-            tt("vt", "v1", "wv", A.min)
-            ts(sn, "vt", -1.0, A.mult, -160.0, A.add)
+        a, b, c = v("pA", R[0:128]), v("pB", R[0:128]), v("pB", R[128:256])
+        ts("xn", win, MAGIC, A.add, -MAGIC, A.add)
+        mm(a, (ONE, "HP"), ("NI", zb), ("I64", "sg"), ("ID", "xn"))
+        mm(b, ("ID", "CH"), ("HI", zb), ("N64", "sg"), ("HI", "xn"))
+        act("r2", a, F.Abs)
+        ts(c, b, MAGIC, A.add, -MAGIC, A.add)
+        tt(sn, c, "r2", A.min)
         trs, lands = [], []
         for c, e in my.items():
             rid, pid, _ = topo.addr(c)
             b = T.rank_of(c)
-            lands.append(v(ln, R[16 * b:16 * b + 16]))
+            lands.append(v(ln, blk(b)))
             trs.append(RemoteDMATransfer(dst_ids=[DstId(rid=rid, pnc=pid)], dma_engine_mask=sum(1 << x for x in e), remote_sem=T.sem["arr%d" % rd],
-                                         src=v(sn, R[16 * b:16 * b + 16])["ap"], dst=v(ln, R[16 * rank:16 * rank + 16])["ap"]))
-        op("G", lambda q: q.remote_dma_fused(trs, local_sem=T.sem.sent), lands, [v(sn)], 0.5, "arr%d" % rd, arrive, 3.5, True)
-        act(v(ln, R[16 * rank:16 * rank + 16]), v(sn, R[16 * rank:16 * rank + 16]))
+                                         src=v(sn, blk(b))["ap"], dst=v(ln, blk(rank))["ap"]))
+        op("G", lambda q: q.remote_dma_fused(trs, local_sem=T.sem.sent), lands, [v(sn)], 0.5, "arr%d" % rd, arrive, 3.0, True)
+        act(v(ln, blk(rank)), v(sn, blk(rank)))
+        tt("fr", win, "xn", A.subtract)
+        if rd < 2:
+            ts("plf", "kj", -512.0, A.add, 0.0, A.max)
 
     def near(rd):
-        spread("pdn", "slN")
-        mm(v("pK", R[256:384]), ("ONE", "NO1"), ("HP", "NO1"), ("ID", "c2"), ("ID", "xn192"))
+        n = 2 if rd < 2 else 1
+        ts("nfr", "fr", -1.0, A.mult)
+        pairs("fr", "nfr", "IT")
+        mm(v("pK", R[256:384]), ("ID", "c2"), ("ID", "xn"))
         ts("vn", v("pK", R[256:384]), 0.0, A.max, 63.0, A.min)
-        if rd < 2:
-            mm(v("pK", R[384:512]), ("I32", "pk"), ("NI", "xn192"), ("ID", "vn"))
-            act("nv", v("pK", R[384:512]), bias=192.0)
+        for b in range(2):
+            ts(v("EQ", R[4 * b:4 * b + 4]), v("pS%d" % b), 1 / 64.0, A.is_equal)
+        mm(v("pD", R[0:128 * n]), ("HI", v("ONE", R[0:128 * n])), sp=False)
+        mm(v("pD", R[0:128]), ("fr", "RS"), st=False, sp=False)
+        for j in range(n):
+            mm(v("pD", R[128 * j:128 * j + 128]), ("sg", "NHI"), st=False, sp=False)
         for k in range(8):
-            compare("EQ" if k < NGR else "GT", "slN", k, "eq" if k < NGR else "sign")
-        if NGR < 8:
-            ts(v("EQ", R[NGR:8]), v("GT", R[NGR:8]), 0.0, A.is_equal, 0.375, A.mult)
-        lowest("pD")
-        a, b = v("pE", R[0:128]), v("pE", R[128:256])
-        mm(v("pE", R[0:256]), ("I32", "CN"), sp=False)
-        mm(b, ("pdn", "RS"), st=False, sp=False)
-        mm(a, ("pk", "S0"), ("xn192", "NS0"), st=False)
-        tt("fn", v("pD", R[0:128]), v("wh", R[128:256]), A.is_lt)
-        offsets("oT", "pE", "fn", "sn", "pD", 2 if rd < 2 else 1)
+            for j in range(n):
+                mm(v("pD", R[128 * j + 16 * k:128 * j + 16 * k + 16]), (v("EQ", k), v("mt", R[16 * k:16 * k + 16])), st=False, sp=k == 7 and j == n - 1)
+        tt(v("sn", R[0:128 * n]), v("pD", R[0:128 * n]), v("DMP", R[0:128 * n]), A.min)
+        for j in range(n):
+            mm(v("pD", R[256 + 8 * j:264 + 8 * j]), (v("sn", R[128 * j:128 * j + 128]), "Q32"))
         if rd < 2:
+            tt(v("pD", R[264:272]), v("pD", R[264:272]), "plf", A.max)
+        cp(v("oT", R[0:8 * n]), v("pD", R[256:256 + 8 * n]))
+        a, b = v("pE", R[384:512]), v("pE", R[256:384])
+        if rd < 2:
+            mm(a, ("ID", "vn"), ("ID", "fr"))
+            act("nv", a)
             cp(ind(XT[rd], v("oT", R[8:16])), "nv")
+            mm(b, ("ID", "vs"), ("ID", "fs"))
+            act(v(XT[rd], R[V:W]), b)
         cp(ind("X", v("oT", R[0:8])), "vn")
         cp(ind("X", v("oS", R[0:8])), "vs")
 
-    for t in range(8):
-        b, cols = v("pS%d" % (t % 2)), R[512 * t:512 * t + 512]
-        if t >= 8 - PACK_S:
-            mm(b, (v("LW", t), "VB"), ("ID", v("X", cols)))
-            act(v("XP", cols), b)
-        else:
-            mm(b, (v("LW", t), "VB"))
-            tt(v("XP", cols), b, v("X", cols), A.add)
-    reorder("XP", "XA", "Wu", FIRST_S)
     for rd in range(3):
-        cands(rd)
+        zb = "z0" if rd == 0 else "land%d" % (rd - 1)
+        cands(rd, zb)
         places(rd)
         if rd == 2:
-            dma("Y", v("seg"), v("XA", R[0:V], p=R[0:128:16]), 2.5)
+            for k in range(2):
+                dma("Y", v("seg", R[256 * k:256 * k + 256]), v("XA", R[0:V], p=R[k:128:16]), 2.5)
             act("sega", "seg", bias=192.0)
-            tt("segf", "seg", "sega", A.subtract)
-            act("Wf", "segf", scale=16384.0, bias=192.0 * 16384)
+            w = v("pE", R[256:512])
+            mm(w, *[x for k in range(2) for x in (("I32", v("seg", R[256 * k:256 * k + 256])), ("NI", v("sega", R[256 * k:256 * k + 256])))])
+            act("Wf", w, scale=16384.0, bias=384.0 * 16384)
             dma("Y", v("XB", R[0:V], p=R[0:128:16]), v("Wf"), 2.5)
-        match(rd)
-        nodes(rd)
+        match(rd, zb)
+        if rd == 2:
+            w = v("pD", R[256:384])
+            mm(w, ("RS", "fs"))
+            act(v("XB", R[V:W]), w, scale=16384.0)
+            reorder("XB", "VAL", "oR", LAST_S)
+            dma("Y", T.yt[:], v("VAL", R[0:V], p=R[0:128:16]), 2.5)
+        nodes(rd, zb)
         near(rd)
         if rd < 2:
             reorder(XT[rd], XT[rd + 1], "oR", MOVE_S)
-            cp(ind(XT[rd + 1], v("oS", R[8:16])), "tv")
-    dma("Y", T.yx[:, 0:2048], v("X", R[0:2048]), 5.0)
-    dma("S", T.yx[:, 2048:V], v("X", R[2048:V]), 6.0)
+    dma("Y", T.yx[:, 0:2048], v("X", R[0:2048]), 4.5)
+    dma("S", T.yx[:, 2048:V], v("X", R[2048:V]), 5.0)
     dma("Y", T.yz[:], v("land2"), 2.0)
-    reorder("XB", "XP", "oR", LAST_S)
-    cp(ind("XP", v("oS", R[8:16])), "tv")
-    dma("S", T.yt[:], v("XP", R[0:V], p=R[0:128:16]), 2.5)
     emit(g, T, arrange(ops))
     g.wait_ge(T.sem.sent, 3 * sum(len(e) for e in my.values()))

@@ -2,7 +2,7 @@ import numpy as np
 from concourse.bass import DstId, RemoteDMATransfer
 from concourse.mybir import AluOpType as A, AxisListType, ActivationFunctionType as F
 
-V, W = 4096, 4224
+V, W, WX = 4096, 4224, 4352
 f32, bf, f16, i32, u16 = "float32", "bfloat16", "float16", "int32", "uint16"
 R = np.s_
 SCRATCH, SHAPE, GROUP = {}, {}, {}
@@ -23,16 +23,17 @@ def _group(name, dtype, width, names):
 
 
 _decl(bf, [W], "X")
-_decl(f32, [W], "XA XB POS")
-_decl(f32, [V], "VAL")
+_decl(f32, [W], "POS")
+_decl(f32, [WX], "XA XB")
+_decl(f32, [V], "VAL VID")
 _decl(bf, [V], "FR D")
 _decl(bf, [32, 4, 2, 16], "AB")
 _decl(bf, [8, 4, 16], "RP4")
 _decl(bf, [512], "REP")
 _decl(bf, [128], "z0 land0 land1 land2 send0 send1 send2 xs")
-_group("gb", bf, 128, "H1 pd npd ad sg c2 vs xn r2 vn fs fr nfr mt first nfm "
+_group("gb", bf, 128, "RN ad sg c2 vs xn r2 vn fs fr mt first nfm "
                       "ID NI HI NHI I64 N64 IX IT NB HP NO1 BO RS IA IB ZE C2K CK CF CP CH C19 TA MA")
-_decl(bf, [8, 128], "SELG EQ GT GU Y")
+_decl(bf, [8, 128], "SELG SELN EQ GT GU Y")
 _group("gc", bf, 256, "RX M16 ONE DH DL")
 _decl(bf, [3, 8, 8, 4], "TW")
 _decl(bf, [3, 8, 32], "TQ")
@@ -45,7 +46,7 @@ _decl(bf, [8, 240], "A0 A1")
 _decl(bf, [8, 264], "SC")
 _decl(bf, [264], "IOC")
 _group("gq", bf, 8, "WQ QA QB")
-_group("gh", f16, 128, "um Pm MB")
+_group("gh", f16, 128, "um Pm MB pd pn")
 _group("gk", f16, 256, "UF CU")
 _group("gf", f32, 128, "I32 CT PRD KAP uu pT S0 tmp rr ww PV0 PV1")
 _group("gg", f32, 256, "sn RST RSC KA KS Wf TF DMP")
@@ -62,18 +63,19 @@ _group("gj", i32, 8, "thr thb kapi ki kj")
 _decl(u16, [256], "Wu Wn oR")
 _decl(u16, [264], "oN")
 _decl(u16, [128], "oC")
+_decl(u16, [32], "oZ")
 _decl(u16, [16], "oS oT su pu")
 _decl(f32, [512], "pA pB pC pD pE pK pS0 pS1", "psum")
-SEMAPHORES = ["sV", "sS", "sP", "sG", "sent", "arr0", "arr1", "arr2"] + ["d%d" % k for k in range(20)]
-LOADS, TURNS, SHAKE = 8, 900, 5.0
-CY, PE, GA, SCA, WAKE = 1.04e-3, 0.52e-3, 1.56, 3.8, 0.1
+SEMAPHORES = ["sV", "sS", "sP", "sG", "sent", "arr0", "arr1", "arr2"] + ["d%d" % k for k in range(28)]
+LOADS, TURNS, SHAKE, SPAN = 8, 3000, 4.0, 4.0
+CY, PE, GA, SCA, WAKE = 0.87e-3, 0.44e-3, 1.56, 3.8, 0.2
 MAGIC = 12582912.0
 STEP_S, STEP_V, HALF = 1, 1, 1
-SCR = 2
+SCR = 6
 SGR = 4
-PLACE_V = 0
-MOVE_S, LAST_S = 14, 12
-CANDS, NODES = ("BBBB", "BBBB", "BBBB"), ("CACAAAAA", "CACAAAAA", "CACAAAAA")
+PLACE = (1,) * 8
+MOVE_S, LAST_S = 16, 12
+CANDS, NODES = ("BBAA", "BBAA", "BBAA"), ("CACAAAAA", "CCBBAAAA", "CACAAAAA")
 REPC, REPN = "VVVV", "VVVV"
 
 
@@ -96,7 +98,7 @@ def masks(topo, src, cores):
     return out
 
 
-def depend(ops):
+def depend(ops, loose=False):
     acc, last, out = {}, {}, []
     for n, o in enumerate(ops):
         hard, soft = set(), set()
@@ -113,9 +115,11 @@ def depend(ops):
                     keep.append((m, had, wr))
             acc[name] = keep
         for bank in o["x"]:
-            if bank in last:
-                (soft if ops[last[bank]]["e"] == o["e"] else hard).add(last[bank])
-            last[bank] = n
+            seen = last.setdefault(bank, [])
+            free = loose and o["free"]
+            for m in seen[:1] if free else seen:
+                (soft if ops[m]["e"] == o["e"] else hard).add(m)
+            last[bank] = seen + [n] if free else [n]
         for name, cols in o["r"]:
             acc.setdefault(name, []).append((n, cols, False))
         for name, cols in o["w"]:
@@ -133,7 +137,7 @@ def arrange(ops):
     n = len(ops)
     if n in ORDER:
         return [ops[k] for k in ORDER[n]]
-    dep = depend(ops)
+    dep = depend(ops, True)
     pre = [[(m, WAKE + ops[m]["lat"]) for m in d[0]] + [(m, 0.0) for m in d[1]] for d in dep]
     for k in range(1, LOADS):
         pre[k].append((k - 1, 0.0))
@@ -171,13 +175,15 @@ def arrange(ops):
     for turn in range(TURNS):
         if turn % 3 == 0:
             key = [-x for x in way] if best is None else list(best[2])
+            seed = (seed * 1103515245 + 12345) % 2 ** 31
+            lo = seed / 2 ** 31 * best[0] - SPAN / 2 if turn else 0.0
             for k in range(n):
                 seed = (seed * 1103515245 + 12345) % 2 ** 31
-                key[k] = max([key[k] + (SHAKE * (seed / 2 ** 31) ** 4 if turn else 0.0)] + [key[m] + 1e-6 for m, lag in pre[k]])
+                key[k] = max([key[k] + (SHAKE * (seed / 2 ** 31) ** 2 if turn and lo < key[k] < lo + SPAN else 0.0)] + [key[m] + 1e-6 for m, lag in pre[k]])
             order = sorted(range(n), key=lambda k: (key[k], k))
         at = place(order, pre, zero)
         end = max(at[k] + c[k] + lat[k] for k in range(n))
-        if best is None or end < best[0]:
+        if best is None or end <= best[0] + 1e-9:
             best = (end, sorted(range(n), key=lambda k: (at[k], k)), at)
         back = place(sorted(range(n), key=lambda k: (-at[k] - c[k], -k)), succ, lat)
         order = sorted(range(n), key=lambda k: (-back[k] - c[k], k))
@@ -203,6 +209,9 @@ def emit(g, T, ops):
         waits.append(ws)
         clock[n] = {} if o["far"] else dict(kn)
         clock[n][o["sem"] or o["e"]] = n
+    ends = {o["sum"]: o for o in ops}
+    for o in ops:
+        o["stop"][0] = ends[o["sum"]] is o
     count, val = {}, {}
     for n, o in enumerate(ops):
         q = eng[o["e"]]
@@ -227,7 +236,7 @@ def rank_program(g, core, T, topo):
     rank = T.rank_of(core)
     if rank is None:
         return
-    ops, ndma, tag, turn = [], [0], [None], [0]
+    ops, ndma, tag, turn, sums = [], [0], [None], [0], {}
 
     def v(name, *idx, p=slice(None)):
         shape, dtype, where = SHAPE[name]
@@ -261,7 +270,8 @@ def rank_program(g, core, T, topo):
                 banks.add(x["k"][0][0])
             if not (x["ps"] and e == "P"):
                 (w if any(x is y for y in outs) else r).extend(x["k"])
-        ops.append({"e": e, "f": f, "r": r, "w": w, "x": sorted(banks), "tag": tag[0], "c": c, "sem": sem, "n": n, "lat": lat, "far": far})
+        ops.append({"e": e, "f": f, "r": r, "w": w, "x": sorted(banks), "tag": tag[0], "c": c, "sem": sem, "n": n, "lat": lat, "far": far,
+                    "free": False, "sum": None, "stop": [False]})
 
     def cost(e, out, a, per):
         if out["ind"] or a["ind"]:
@@ -311,11 +321,18 @@ def rank_program(g, core, T, topo):
         else:
             ts(out, a, c, A.add)
 
-    def mm(out, *terms, st=True, sp=True):
-        for j, (l, rr) in enumerate(terms):
-            l, rr = u(l), u(rr)
-            a, b = st and j == 0, sp and j == len(terms) - 1
-            op("P", lambda q, l=l, rr=rr, a=a, b=b: q.matmul(out["ap"], l["ap"], rr["ap"], a, b), [out], [l, rr], max(64, rr["n"]) * (4 if l["f32"] else 1) * PE)
+    def mm(out, *terms, st=True, sp=True, hold=False, run=False):
+        terms = [(u(x[0]), u(x[1]), x[2] if len(x) > 2 else out) for x in terms]
+        bank = terms[0][2]["k"][0][0]
+        runs = [terms] if run else [[x] for x in terms]
+        for j, xs in enumerate(runs):
+            a, b = st and j == 0, [False]
+            sums[bank] = sums.get(bank, 0) + a
+
+            def f(q, xs=xs, a=a, b=b):
+                return [q.matmul(o["ap"], l["ap"], rr["ap"], a and k == 0, b[0] and k == len(xs) - 1) for k, (l, rr, o) in enumerate(xs)][-1]
+            op("P", f, [xs[0][2]], [y for x in xs for y in x[:2]], sum(max(64, rr["n"]) * (4 if l["f32"] else 1) * PE for l, rr, o in xs))
+            ops[-1].update({"free": not a and not (hold and j == len(runs) - 1), "sum": (bank, sums[bank]), "stop": b})
 
     def iota(out, pat, base, cm=0):
         out = u(out)
@@ -340,15 +357,14 @@ def rank_program(g, core, T, topo):
     dma("Y", v("X", R[2048:V]), T.xr[:, 2048:V], 6.5)
 
     cp("Wn", "TN")
-    for t in range(8):
-        off = ind("POS", v("Wn", R[32 * t:32 * t + 32]), V)
-        tag[0] = "place"
-        if t < 8 - PLACE_V:
-            iota(v("VAL", R[512 * t:512 * t + 512]), [[1, 32], [256, 16]], 64 + 32 * t)
-            act(off, v("VAL", R[512 * t:512 * t + 512]), F.Silu)
-        else:
-            ts(off, v("VAL", R[0:512]), 1.0, A.mult, 32.0 * t, A.add)
-        tag[0] = None
+    t = 0
+    for k in PLACE:
+        for j in range(t, t + k):
+            iota(v("VAL", R[512 * j:512 * j + 512]), [[1, 32], [256, 16]], 56 + 32 * j)
+        act(ind("POS", v("Wn", R[32 * t:32 * (t + k)]), V), v("VAL", R[512 * t:512 * (t + k)]), F.Silu)
+        t += k
+    for t in range(t, 8):
+        ts(ind("POS", v("Wn", R[32 * t:32 * t + 32]), V), v("VAL", R[0:512]), 1.0, A.mult, 32.0 * t, A.add)
 
     ms("ONE", 1.0)
     for n, c in (("HP", 0.5), ("NO1", -1.0), ("CT", 0.0), ("C2K", 2048.0)):
@@ -366,17 +382,20 @@ def rank_program(g, core, T, topo):
     iota(v("CT", R[0:16:2]), [[1, 8]], 1)
     iota(v("CT", R[1:14:2]), [[-1, 7]], 7)
     iota(c1("CT", 15), [[0, 1]], 1)
-    iota(v("CT", R[16:18]), [[0, 2]], 1)
-    iota(c1("CT", 33), [[0, 1]], 1)
-    iota(v("CT", R[48:64]), [[1, 16]], 0)
+    iota(v("CT", R[16:32]), [[0, 2], [1, 8]], 0)
+    iota(v("CT", R[32:48]), [[1, 16]], 0)
     ts("q0", "mi", 15, A.bitwise_and)
     for k in range(2):
         ts(v("M16", R[128 * k:128 * k + 128]), "q0", 0.0, A.is_equal)
-    tt(v("PRD", R[0:64]), v("CT", R[0:64]), v("M16", R[0:64]), A.mult)
-    for k in range(4):
+    tt(v("PRD", R[0:48]), v("CT", R[0:48]), v("M16", R[0:48]), A.mult)
+    for k in range(3):
         red(col[k], v("PRD", R[16 * k:16 * k + 16]))
-    for n in ("X", "XA", "XB", "POS"):
-        iota(v(n, R[V:W]), [[0, W - V]], 0)
+    ts(col[3], col[1], 8196.5, A.add)
+    if "S" in (REPC, REPN):
+        iota(v("rr", R[0:32]), [[16, 8], [0, 4]], 0)
+        ts("oZ", v("rr", R[0:32]), col[2], A.add)
+    for t in range(8):
+        iota(v("VID", R[512 * t:512 * t + 512]), [[1, 512]], 512 * t)
     ms(c1("ac", 0), -0.375)
     cp("I32", "ID")
     cp(c1("cc", 0), c1("kapi", 0))
@@ -391,34 +410,37 @@ def rank_program(g, core, T, topo):
         if need:
             iota(n, [[0, 144]], 0)
             ts(v(n, R[15:128:16]), Q, c, A.mult)
-    for n, c in (("NI", -1.0), ("HI", 0.5), ("NHI", -0.5), ("I64", 64.0), ("N64", -64.0), ("IX", 32.0), ("IT", 1 / 64.0), ("NB", -2.0 ** 23),
-                 ("IA", 1032.0 * 8192), ("IB", -2040.0 * 8192)):
+    for n, c in (("NI", -1.0), ("HI", 0.5), ("NHI", -0.5), ("I64", 64.0), ("N64", -64.0), ("IX", 32.0), ("IT", -2.0 ** -11), ("NB", -2.0 ** 23),
+                 ("IA", 1032.0 * 8192), ("IB", -2040.0 * 8192))[:10 if "B" in both[1] else 8]:
         sel(n, "ZE", [[-1, 128]], A.not_equal, 0, 1, c)
     for n, c in (("MA", -1664.0), ("MB", 2047.0)):
         ts(n, M16, c, A.mult)
     WB = v("RX", R[0:128])
     for n, c in ((WB, 1.0), (v("RX", R[128:256]), 0.0625)):
         ts(n, "BO", col[0], A.mult, c, A.mult)
-    sel("RS", "BO", [[16, 8], [0, 16]], A.is_ge, 1, -1)
-    for n, c in (("CK", -504 * 32768), ("CP", -2112), ("C19", 2 ** 19), (v("CU", R[0:128]), -2047), (v("CU", R[128:256]), 1536),
-                 ("PV0", V + 64), ("PV1", V + 192)):
+    for n, c in (("RS", 2.0 ** -4), ("RN", 2.0 ** -18)):
+        ts(n, "BO", c, A.mult)
+    for n, c in (("CK", -504 * 32768), ("CP", -10304), ("C19", 2 ** 19), (v("CU", R[0:128]), -2047), (v("CU", R[128:256]), 1536),
+                 ("PV0", V + 56), ("PV1", V + 184)):
         iota(n, [[1 if n in ("PV0", "PV1") else 0, 128]], c)
     for n, c in (("CF", -15 / 32.0), ("CH", 63.75)):
         ms(n, c)
-    ts("thq", Q, col[1], A.mult, 512.0, A.mult)
-    cp("WQ", "thq")
+    ts("WQ", Q, 32.0, A.mult)
     for k in range(8):
-        ts(v("SELG", k), ONE, c1("thq", k), A.mult)
+        ts(v("SELG", k), ONE, c1("WQ", k), A.mult)
+    ts("SELN", "SELG", -1.0, A.mult)
     iota(c1("cc", 2), [[0, 1]], 0, 1)
     ts("Q32", Q, 16384.0, A.mult)
     ts("QA", Q, 4096.0, A.mult)
     ts("QB", Q, c1("cc", 2), A.mult)
-    iota(v("dc", R[0:2]), [[128, 2]], V + 64, 1)
+    iota(v("dc", R[0:2]), [[128, 2]], V + 8256, 1)
     ts(v("dc", R[2:4]), v("dc", R[0:2]), 512.0, A.mult)
     ts(c1("dc", 4), c1("cc", 2), 2.0 ** -14, A.mult, 0.25, A.add)
-    ts("DMP", "M16", c1("dc", 4), A.mult)
+    ts(c1("dc", 5), c1("dc", 4), 2.0 ** -7, A.add)
+    for k in range(2):
+        ts(v("DMP", R[128 * k:128 * k + 128]), M16, c1("dc", 4 + k), A.mult)
     ts(c1("cc", 7), c1("cc", 2), 16.0 * SCR, A.is_ge, 64.0, A.mult)
-    tt(c1("cc", 6), c1("cc", 7), col[3], A.add)
+    tt(c1("cc", 6), c1("cc", 7), col[2], A.add)
     for j, (s, base) in enumerate(((0, 1), (-1, 0), (16, 0))):
         iota(v("KW", j), [[s, 32]], base)
         iota(v("KQ", j), [[s, 4], [4 * s, 2], [8 * s, 4]], base)
@@ -433,9 +455,13 @@ def rank_program(g, core, T, topo):
     iota("TA", [[0, 128]], -256)
     sel("TA", "TA", [[-1, 128]], A.is_gt, 0, 1)
     sel("TRI", ONE, [[1, 128]], A.is_gt, 0, -1)
-    for k in range(4):
-        iota(v("A0", R[2 * k:2 * k + 2]), [[0, 480]], 0)
+    ms(v("A0", 0), 0.0)
+    for k in (1, 2, 4):
+        dma("Y", v("A0", R[k:2 * k]), v("A0", R[0:k]), 2.5)
     dma("Y", v("A1"), v("A0"), 2.5)
+    dma("Y", v("X", R[V:W]), v("ZE"), 2.0)
+    for n, w in (("XA", WX), ("XB", WX), ("POS", W)):
+        dma("Y", v(n, R[V:w]), v("RSC", R[0:w - V]), 2.0)
     ts("osf", Q, 1.0, A.mult)
     tt("plf", "thb", "osf", A.mult)
     red(c1("cc", 1), "plf")
@@ -469,6 +495,9 @@ def rank_program(g, core, T, topo):
         return v("pK", R[n // 2 * (c % 2) + c // 2:32 * n:n])
 
     def repeat(engines, src, c):
+        if engines == "S":
+            act("REP", ind(src, v("oZ"), 128), bias=c)
+            return
         for k in range(4):
             shift(engines[k], v("RP4", R[:, k]), src, c)
         cp("REP", "RP4")
@@ -494,14 +523,16 @@ def rank_program(g, core, T, topo):
                 ts(size, d, 0.0, A.max, 2.0, A.mult)
         b, n = c // 2, len(hows)
 
-        def sums(out, z, rhs, stop):
-            mm(out, *[(v(z, R[15 - r:143 - r]), rhs(r)) for r in range(16)], st=False, sp=stop)
+        def add(out, z, rhs):
+            mm(out, *[(v(z, R[15 - r:143 - r]), rhs(r)) for r in range(16)], st=False, run=True)
+        tag[0] = ("pair", b) if bias and "B" in hows[2 * b:2 * b + 2] else None
         if how == "B":
-            sums(piece(c, n), zz[2], lambda r: v("D", R[512 * c + r:512 * c + 512:16]), False)
+            add(piece(c, n), zz[2], lambda r: v("D", R[512 * c + r:512 * c + 512:16]))
         if (hows[2 * b] == "B") != (hows[2 * b + 1] == "B"):
-            sums(piece(c, n), zz[how == "B"], lambda r: v("AB", R[8 * b:8 * b + 8, :, c % 2, r]), c == n - 1)
+            add(piece(c, n), zz[how == "B"], lambda r: v("AB", R[8 * b:8 * b + 8, :, c % 2, r]))
         elif c % 2:
-            sums(v("pK", R[b:32 * n:n // 2]), zz[how == "B"], lambda r: v("AB", R[8 * b:8 * b + 8, :, :, r]), c == n - 1)
+            add(v("pK", R[b:32 * n:n // 2]), zz[how == "B"], lambda r: v("AB", R[8 * b:8 * b + 8, :, :, r]))
+        tag[0] = None
 
     def reorder(src, dst, lst, on_s):
         t = 0
@@ -541,18 +572,20 @@ def rank_program(g, core, T, topo):
     def bank4(k):
         return v("pS%d" % (k // 4), R[128 * (k % 4):128 * (k % 4) + 128])
 
-    def pairs(digits, minus, tri):
+    def pairs(digits):
         for b in range(2):
-            for k in range(4 * b, 4 * b + 4):
-                mm(bank4(k), (tri, "TRI"), st=k % 4 == 0, sp=False)
-            for k in range(4 * b, 4 * b + 4):
-                mm(bank4(k), (v("SELG", k), digits), (minus, v("SELG", k)), st=False, sp=k % 4 == 3)
+            ks = range(4 * b, 4 * b + 4)
+            mm(None, *[("ID", "TRI", bank4(k)) for k in ks], run=True)
+            mm(None, *[x for k in ks for x in ((v("SELG", k), digits, bank4(k)), (digits, v("SELN", k), bank4(k)))], st=False, run=True)
+
+    def by_group(bank, buf, rhs, at=0):
+        for b in range(2):
+            mm(None, *[(v(buf, k), v(rhs, R[16 * k:16 * k + 16]), v(bank, R[at + 16 * k:at + 16 * k + 16])) for k in range(4 * b, 4 * b + 4)], st=False, run=True)
 
     def places(rd):
         sl, P = v("su", R[0:8]), v("pA", R[0:128])
-        cp("xs", ind("X", sl))
-        act("H1", ind("POS", sl), scale=col[2])
-        tt("pd", ind("POS", sl), "H1", A.subtract)
+        ts("pd", ind("POS", sl), col[3], A.add)
+        act("xs", ind("X", sl))
         n1, n2, n3, kn = v("pC", R[0:64]), v("pE", R[0:192]), v("pE", R[192:200]), v("pK", R[0:256])
         tw = lambda j, a, b: v("TW", R[j, a // 32:b // 32])
         tq = lambda j: v("TQ", j)
@@ -567,8 +600,8 @@ def rank_program(g, core, T, topo):
         mm(P, ("ID", "CP"), sp=False)
         if rd:
             mm(v("pA", R[16 * SGR:128]), *[("HP", v("NO1", R[16 * SGR:128]))] * rd, st=False, sp=False)
-            for k in range(8):
-                mm(bank4(k), (v("SELG", k), "pd"))
+            for b in (1, 0):
+                mm(None, *[(v("SELG", k), "pd", bank4(k)) for k in range(4 * b, 4 * b + 4)], run=True)
         mm(P, ("pd", "RS"), st=False, sp=rd == 0)
         repeat(REPN, "xs", -192.0)
         for s in range(rd):
@@ -578,17 +611,17 @@ def rank_program(g, core, T, topo):
                     ts(v(buf, k), bank4(k), c1("RT%d" % s, k), A.is_gt)
                 else:
                     act(v(buf, k), bank4(k), F.Sign, scale=-1.0, bias=c1("RT%d" % s, k))
-            for k in (0, 4, 1, 5, 2, 6, 3, 7):
-                mm(v("pA", R[16 * k:16 * k + 16]), (v(buf, k), v("NO1" if k < SGR else "HP", R[0:16])), st=False, sp=s == rd - 1 and k == 7)
+            for k0 in range(0, 8, 2):
+                mm(None, *[(v(buf, k), v("NO1" if k < SGR else "HP", R[0:16]), v("pA", R[16 * k:16 * k + 16])) for k in (k0, k0 + 1)], st=False, run=True)
         tt("UF", v("pB", R[0:256]), "M16", A.mult)
         tt("Pm", P, M16, A.mult)
         Um, Fm = v("UF", R[0:128]), v("UF", R[128:256])
         mm(n1, (Um, tw(1, 0, 64)), (Fm, tw(2, 0, 64)), ("Pm", tw(0, 0, 64)), st=False)
         mm(n2, (Um, tw(1, 64, 256)), (Fm, tw(2, 64, 256)), ("Pm", tw(0, 64, 256)), st=False, sp=False)
         mm(n3, ("Pm", Q), st=False)
-        mm(kn, (Um, tq(1)), (Fm, tq(2)), ("Pm", tq(0)), st=False, sp=False)
-        for c in range(8) if "B" in NODES[rd] else ():
-            mm(piece(c, 8), ("IB" if NODES[rd][c] == "B" else "IA", v("ONE", R[0:32])), st=False, sp=False)
+        mm(kn, (Um, tq(1)), (Fm, tq(2)), ("Pm", tq(0)), st=False, hold=True)
+        if "B" in NODES[rd]:
+            mm(None, *[("IB" if NODES[rd][c] == "B" else "IA", v("ONE", R[0:32]), piece(c, 8)) for c in range(8)], st=False, hold=True, run=True)
         cp(v("oN", R[0:64]), n1)
         cp(v("oN", R[64:264]), v("pE", R[0:200]))
         act("pT", P, scale=-256.0)
@@ -597,7 +630,6 @@ def rank_program(g, core, T, topo):
         d0, d1, d2, d3 = (v("pD", R[128 * k:128 * k + 128]) for k in range(4))
         mm(d0, ("ID", zb), ("NI", "xs"))
         act("ad", d0, F.Abs)
-        ts("c2", d0, -2.0, A.max, 2.0, A.min)
         mm(d2, ("BO", "ad"))
         act("sg", d2, F.Sign, c1("cc", 5), scale=-1.0, bias=c1("th", rd))
         if rd < 2:
@@ -605,16 +637,15 @@ def rank_program(g, core, T, topo):
             act(c1("th", rd + 1), c1("cc", 5), scale=-0.5, bias=c1("th", 3))
         mm(d3, ("sg", "ID"))
         act("mt", d3, F.Relu)
-        mm(d1, ("NHI", "HP"), ("HI", zb), ("HI", "xs"))
+        mm(d1, ("NHI", "HP"), ("HI", zb), ("HI", "xs"), run=True)
+        ts("c2", d0, -2.0, A.max, 2.0, A.min)
         ts("vs", d1, MAGIC, A.add, -MAGIC, A.add)
         tt("fs", ind(XT[rd], v("oN", R[256:264])), "xs", A.subtract)
-        ts("npd", "pd", -1.0, A.mult)
-        pairs("pd", "npd", "ID")
+        pairs("pd")
         for b in range(2):
             ts(v("Y", R[4 * b:4 * b + 4]), v("pS%d" % b), 0.0, A.max, 256.0, A.min)
-        mm(d0, ("HI", ONE), ("sg", "NHI"), sp=False)
-        for k in range(8):
-            mm(v("pD", R[16 * k:16 * k + 16]), (v("Y", k), v("mt", R[16 * k:16 * k + 16])), st=False, sp=k == 7)
+        mm(d0, ("HI", ONE), ("sg", "NHI"), run=True)
+        by_group("pD", "Y", "mt")
         ts("rr", d0, 256 * MAGIC, A.add, -256 * MAGIC, A.add)
         tt("first", d0, "rr", A.is_equal)
         tt("nfm", "first", M16, A.is_lt)
@@ -628,10 +659,9 @@ def rank_program(g, core, T, topo):
             ts("RT%d" % rd, w, c1("dc", 2 + rd), A.min)
             act(ind("POS", v("oS", R[0:8])), "PV%d" % rd, F.Silu)
         a, b = v("pC", R[0:128]), v("pC", R[128:256])
-        mm(b, ("ID", "C19"), ("ID", "C19"), (ONE, ONE), ("TA", "first"), sp=False)
-        mm(a, ("ID", "C19"), ("I32", "pT"), ("TA", "first"), st=False, sp=False)
-        for k in range(8):
-            mm(v("pC", R[16 * k:16 * k + 16]), (v("Y", k), v("first", R[16 * k:16 * k + 16])), st=False, sp=k == 7)
+        mm(b, ("ID", "C19"), ("ID", "C19"), (ONE, ONE), ("ID", "C19", a), ("I32", "pT", a), run=True)
+        mm(b, ("TA", "first"), ("TA", "first", a), st=False, run=True)
+        by_group("pC", "Y", "first")
         tt("ww", a, "first", A.mult)
         tt("ti", b, "ww", A.subtract)
         if SCR < 8:
@@ -646,10 +676,10 @@ def rank_program(g, core, T, topo):
                 act(v("SC", R[k, 0:257]), v("IOC", R[0:257]), F.Sign, bias=c1("ntc", k))
         tt(v("A1", R[:, 112:128]), "tr", "r1", A.is_le)
         ts(v("A0", R[:, 112:128]), v("A1", R[:, 112:128]), -1.0, A.mult, 1.0, A.add)
-        terms = [("IX", v("IOC", R[1:257]))]
+        mm(v("pE", R[0:256]), ("IX", v("IOC", R[1:257])))
         for k in range(8):
-            terms += [(v("A1", R[k, 112 - 16 * k:240 - 16 * k]), v("SC", R[k, 1:257])), (v("A0", R[k, 112 - 16 * k:240 - 16 * k]), v("SC", R[k, 0:256]))]
-        mm(v("pE", R[0:256]), *terms)
+            mm(v("pE", R[0:256]), (v("A1", R[k, 112 - 16 * k:240 - 16 * k]), v("SC", R[k, 1:257])),
+               (v("A0", R[k, 112 - 16 * k:240 - 16 * k]), v("SC", R[k, 0:256])), st=False, run=True)
         ts("oR", v("pE", R[0:256]), 0.5, A.mult, c1("cc", 6), A.add)
 
     def nodes(rd, zb):
@@ -679,38 +709,32 @@ def rank_program(g, core, T, topo):
                                          src=v(sn, blk(b))["ap"], dst=v(ln, blk(rank))["ap"]))
         op("G", lambda q: q.remote_dma_fused(trs, local_sem=T.sem.sent), lands, [v(sn)], 0.5, "arr%d" % rd, arrive, 3.0, True)
         act(v(ln, blk(rank)), v(sn, blk(rank)))
+        ts("pn", ind("VID", pl, V), col[3], A.add)
         tt("fr", win, "xn", A.subtract)
-        if rd < 2:
-            ts("plf", "kj", -512.0, A.add, 0.0, A.max)
 
     def near(rd):
         n = 2 if rd < 2 else 1
-        ts("nfr", "fr", -1.0, A.mult)
-        pairs("fr", "nfr", "IT")
+        pairs("pn")
         mm(v("pK", R[256:384]), ("ID", "c2"), ("ID", "xn"))
         ts("vn", v("pK", R[256:384]), 0.0, A.max, 63.0, A.min)
         for b in range(2):
-            ts(v("EQ", R[4 * b:4 * b + 4]), v("pS%d" % b), 1 / 64.0, A.is_equal)
-        mm(v("pD", R[0:128 * n]), ("HI", v("ONE", R[0:128 * n])), sp=False)
-        mm(v("pD", R[0:128]), ("fr", "RS"), st=False, sp=False)
-        for j in range(n):
-            mm(v("pD", R[128 * j:128 * j + 128]), ("sg", "NHI"), st=False, sp=False)
-        for k in range(8):
-            for j in range(n):
-                mm(v("pD", R[128 * j + 16 * k:128 * j + 16 * k + 16]), (v("EQ", k), v("mt", R[16 * k:16 * k + 16])), st=False, sp=k == 7 and j == n - 1)
-        tt(v("sn", R[0:128 * n]), v("pD", R[0:128 * n]), v("DMP", R[0:128 * n]), A.min)
-        for j in range(n):
-            mm(v("pD", R[256 + 8 * j:264 + 8 * j]), (v("sn", R[128 * j:128 * j + 128]), "Q32"))
+            ts(v("EQ", R[4 * b:4 * b + 4]), v("pS%d" % b), 1.0, A.is_equal)
+        mm(v("pD", R[0:128]), ("HI", ONE), ("fr", "BO"), sp=False)
         if rd < 2:
-            tt(v("pD", R[264:272]), v("pD", R[264:272]), "plf", A.max)
+            mm(v("pD", R[128:256]), ("IT", ONE), ("pn", "RN"), st=False, sp=False)
+        for j in range(n):
+            mm(v("pD", R[128 * j:128 * j + 128]), ("sg", "NHI"), st=False)
+            by_group("pD", "EQ", "mt", 128 * j)
+        tt(v("sn", R[0:128 * n]), v("pD", R[0:128 * n]), v("DMP", R[0:128 * n]), A.min)
+        mm(None, *[(v("sn", R[128 * j:128 * j + 128]), "Q32", v("pD", R[256 + 8 * j:264 + 8 * j])) for j in range(n)], run=True)
         cp(v("oT", R[0:8 * n]), v("pD", R[256:256 + 8 * n]))
-        a, b = v("pE", R[384:512]), v("pE", R[256:384])
+        a, b = v("pK", R[384:512]), v("pA", R[128:256])
         if rd < 2:
             mm(a, ("ID", "vn"), ("ID", "fr"))
             act("nv", a)
-            cp(ind(XT[rd], v("oT", R[8:16])), "nv")
             mm(b, ("ID", "vs"), ("ID", "fs"))
             act(v(XT[rd], R[V:W]), b)
+            cp(ind(XT[rd], v("oT", R[8:16]), WX), "nv")
         cp(ind("X", v("oT", R[0:8])), "vn")
         cp(ind("X", v("oS", R[0:8])), "vs")
 
@@ -729,10 +753,10 @@ def rank_program(g, core, T, topo):
         match(rd, zb)
         if rd == 2:
             w = v("pD", R[256:384])
-            mm(w, ("RS", "fs"))
+            mm(w, ("BO", "fs"))
             act(v("XB", R[V:W]), w, scale=16384.0)
-            reorder("XB", "VAL", "oR", LAST_S)
-            dma("Y", T.yt[:], v("VAL", R[0:V], p=R[0:128:16]), 2.5)
+            reorder("XB", "POS", "oR", LAST_S)
+            dma("Y", T.yt[:], v("POS", R[0:V], p=R[0:128:16]), 2.5)
         nodes(rd, zb)
         near(rd)
         if rd < 2:

import numpy as np
from concourse.bass import DstId, RemoteDMATransfer
from concourse.mybir import AluOpType as A, AxisListType, ActivationFunctionType as F

V, W, WX = 4096, 4224, 4352
f32, bf, f16, i32, u16 = "float32", "bfloat16", "float16", "int32", "uint16"
R = np.s_
SCRATCH, SHAPE, GROUP = {}, {}, {}


def _decl(dtype, shape, names, where="sbuf"):
    for n in names.split():
        SCRATCH[n] = (where, [128] + shape, dtype)
        SHAPE[n] = (shape, dtype, where)


def _group(name, dtype, width, names):
    names = names.split()
    SCRATCH[name] = ("sbuf", [128, len(names), width], dtype)
    for k, n in enumerate(names):
        GROUP[n] = (name, k)
        SHAPE[n] = ([width], dtype, "sbuf")


_decl(bf, [W], "X")
_decl(f32, [W], "POS")
_decl(f32, [WX], "XA XB")
_decl(f32, [V], "VAL VID")
_decl(bf, [V], "FR D")
_decl(bf, [32, 4, 2, 16], "AB")
_decl(bf, [8, 4, 16], "RP4")
_decl(bf, [512], "REP")
_decl(bf, [128], "z0 land0 land1 land2 send0 send1 send2 xs")
_group("gb", bf, 128, "RN ad sg c2 vs xn r2 vn fs fr mt first nfm "
                      "ID NI HI NHI I64 N64 IX IT NB HP NO1 BO RS IA IB ZE C2K CK CF CP CH C19 TA MA")
_decl(bf, [8, 128], "SELG SELN EQ GT GU Y")
_group("gc", bf, 256, "RX M16 ONE DH DL")
_decl(bf, [3, 8, 8, 4], "TW")
_decl(bf, [3, 8, 32], "TQ")
_decl(bf, [3, 32], "KW KQ")
_decl(bf, [128], "TRI")
_decl(bf, [512], "sega")
_decl(f32, [128], "nv")
_group("gz", bf, 144, "Z1 Z1n Z2 Z2b Z2p")
_decl(bf, [8, 240], "A0 A1")
_decl(bf, [8, 264], "SC")
_decl(bf, [264], "IOC")
_group("gq", bf, 8, "WQ QA QB")
_group("gh", f16, 128, "um Pm MB pd pn")
_group("gk", f16, 256, "UF CU")
_group("gf", f32, 128, "I32 CT PRD KAP uu pT S0 tmp rr ww PV0 PV1")
_group("gg", f32, 256, "sn RST RSC KA KS Wf TF DMP")
_decl(f32, [512], "seg")
_decl(f32, [8, 16], "PA PB")
_decl(i32, [8, 32], "M")
_decl(i32, [8, 32], "Mt")
_group("ge", f32, 8, "col sW osf plf RT0 RT1 tc ntc Q32 thq cc ac th dc")
_group("gi", i32, 128, "mi q0 sum ti tr r1")
_decl(i32, [8, 16], "h")
_decl(i32, [2, 128], "L")
_decl(i32, [256], "TN")
_group("gj", i32, 8, "thr thb kapi ki kj")
_decl(u16, [256], "Wu Wn oR")
_decl(u16, [264], "oN")
_decl(u16, [128], "oC")
_decl(u16, [32], "oZ")
_decl(u16, [16], "oS oT su pu")
_decl(f32, [512], "pA pB pC pD pE pK pS0 pS1", "psum")
SEMAPHORES = ["sV", "sS", "sP", "sG", "sent", "arr0", "arr1", "arr2"] + ["d%d" % k for k in range(28)]
LOADS, TURNS, SHAKE, SPAN = 8, 3000, 4.0, 4.0
CY, PE, GA, SCA, WAKE = 0.87e-3, 0.44e-3, 1.56, 3.8, 0.2
MAGIC = 12582912.0
STEP_S, STEP_V, HALF = 1, 1, 1
SCR = 6
SGR = 4
PLACE = (1,) * 8
MOVE_S, LAST_S = 16, 12
CANDS, NODES = ("BBAA", "BBAA", "BBAA"), ("CACAAAAA", "CCBBAAAA", "CACAAAAA")
REPC, REPN = "VVVV", "VVVV"


def masks(topo, src, cores):
    far = [c for c in cores if topo.chip(c) != topo.chip(src)]
    near = [c for c in cores if c != src and c not in far]
    fe = topo.engines(src, far[0])
    ne = [e for e in topo.engines(src, near[0]) if e not in fe]
    out = {}
    for dsts, eng in ((far, fe), (near, ne)):
        share = [1] * len(dsts)
        k = 0
        while sum(share) + share[k % len(dsts)] <= len(eng):
            share[k % len(dsts)] *= 2
            k += 1
        at = 0
        for c, n in zip(dsts, share):
            out[c] = eng[at:at + n]
            at += n
    return out


def depend(ops, loose=False):
    acc, last, out = {}, {}, []
    for n, o in enumerate(ops):
        hard, soft = set(), set()
        for name, cols in o["r"]:
            for m, had, wr in acc.get(name, []):
                if wr and had & cols:
                    hard.add(m)
        for name, cols in o["w"]:
            keep = []
            for m, had, wr in acc.get(name, []):
                if had & cols:
                    hard.add(m)
                if had & ~cols:
                    keep.append((m, had, wr))
            acc[name] = keep
        for bank in o["x"]:
            seen = last.setdefault(bank, [])
            free = loose and o["free"]
            for m in seen[:1] if free else seen:
                (soft if ops[m]["e"] == o["e"] else hard).add(m)
            last[bank] = seen + [n] if free else [n]
        for name, cols in o["r"]:
            acc.setdefault(name, []).append((n, cols, False))
        for name, cols in o["w"]:
            acc[name].append((n, cols, True))
        hard.discard(n)
        soft.discard(n)
        out.append((hard, soft - hard))
    return out


ORDER = {}


def arrange(ops):
    n = len(ops)
    if n in ORDER:
        return [ops[k] for k in ORDER[n]]
    dep = depend(ops, True)
    pre = [[(m, WAKE + ops[m]["lat"]) for m in d[0]] + [(m, 0.0) for m in d[1]] for d in dep]
    for k in range(1, LOADS):
        pre[k].append((k - 1, 0.0))
    seen = {}
    for k, o in enumerate(ops):
        if o["tag"]:
            if (o["tag"], o["e"]) in seen:
                pre[k].append((seen[o["tag"], o["e"]], 0.0))
            seen[o["tag"], o["e"]] = k
    succ = [[] for _ in ops]
    for k in range(n):
        for m, lag in pre[k]:
            succ[m].append((k, lag))
    c, eng = [o["c"] for o in ops], [o["e"] for o in ops]

    def place(order, before, first):
        busy, at = {e: [] for e in "VSPGY"}, [0.0] * n
        for k in order:
            t = max([at[m] + c[m] + lag for m, lag in before[k]] + [first[k]])
            b = busy[eng[k]]
            j = len(b)
            while j and b[j - 1][1] > t:
                j -= 1
            while j < len(b) and b[j][0] < t + c[k]:
                t = max(t, b[j][1])
                j += 1
            b.insert(j, (t, t + c[k]))
            at[k] = t
        return at
    lat, zero = [o["lat"] for o in ops], [0.0] * n
    way = [0.0] * n
    for k in range(n - 1, -1, -1):
        way[k] = c[k] + max([way[s] + lag for s, lag in succ[k]] + [lat[k]])
    best, seed = None, 1
    for turn in range(TURNS):
        if turn % 3 == 0:
            key = [-x for x in way] if best is None else list(best[2])
            seed = (seed * 1103515245 + 12345) % 2 ** 31
            lo = seed / 2 ** 31 * best[0] - SPAN / 2 if turn else 0.0
            for k in range(n):
                seed = (seed * 1103515245 + 12345) % 2 ** 31
                key[k] = max([key[k] + (SHAKE * (seed / 2 ** 31) ** 2 if turn and lo < key[k] < lo + SPAN else 0.0)] + [key[m] + 1e-6 for m, lag in pre[k]])
            order = sorted(range(n), key=lambda k: (key[k], k))
        at = place(order, pre, zero)
        end = max(at[k] + c[k] + lat[k] for k in range(n))
        if best is None or end <= best[0] + 1e-9:
            best = (end, sorted(range(n), key=lambda k: (at[k], k)), at)
        back = place(sorted(range(n), key=lambda k: (-at[k] - c[k], -k)), succ, lat)
        order = sorted(range(n), key=lambda k: (-back[k] - c[k], k))
    ORDER[n] = best[1]
    ORDER["end"] = best[0]
    return [ops[k] for k in best[1]]


def emit(g, T, ops):
    eng = {"V": g.vector, "S": g.scalar, "P": g.tensor, "G": g, "Y": g.sync}
    known = {e: {} for e in eng}
    clock, waits, need = {}, [], set()
    for n, (o, (d, _)) in enumerate(zip(ops, depend(ops))):
        kn = known[o["e"]]
        ws = []
        for m in sorted(d, reverse=True):
            if kn.get(ops[m]["sem"] or ops[m]["e"], -1) >= m:
                continue
            ws.append(m)
            need.add(m)
            for c, x in clock[m].items():
                kn[c] = max(kn.get(c, -1), x)
        waits.append(ws)
        clock[n] = {} if o["far"] else dict(kn)
        clock[n][o["sem"] or o["e"]] = n
    ends = {o["sum"]: o for o in ops}
    for o in ops:
        o["stop"][0] = ends[o["sum"]] is o
    count, val = {}, {}
    for n, o in enumerate(ops):
        q = eng[o["e"]]
        for m in waits[n]:
            q.wait_ge(T.sem[val[m][0]], val[m][1])
        ins = o["f"](q)
        if o["sem"]:
            val[n] = (o["sem"], o["n"])
            count[o["sem"]] = o["n"]
            if not o["far"]:
                ins.then_inc(T.sem[o["sem"]], 16)
        elif n in need:
            s = "s" + o["e"]
            count[s] = count.get(s, 0) + 1
            val[n] = (s, count[s])
            ins.then_inc(T.sem[s], 1)
    for s, c in count.items():
        g.wait_ge(T.sem[s], c)


def rank_program(g, core, T, topo):
    rank = T.rank_of(core)
    if rank is None:
        return
    ops, ndma, tag, turn, sums = [], [0], [None], [0], {}

    def v(name, *idx, p=slice(None)):
        shape, dtype, where = SHAPE[name]
        if len(idx) == 1 and isinstance(idx[0], tuple):
            idx = idx[0]
        at = np.arange(int(np.prod(shape))).reshape(shape)[idx]
        ap = T[GROUP[name][0]][(p, GROUP[name][1]) + (idx or (slice(None),))] if name in GROUP else T[name][(p,) + idx]
        used = np.zeros(int(np.prod(shape)), np.uint8)
        used[np.ravel(at)] = 1
        span = (name, int.from_bytes(bytes(np.packbits(used)), "big"))
        return {"ap": ap, "n": int(np.size(at)), "k": [span], "two": dtype in (bf, f16, u16), "ps": where == "psum", "f32": dtype == f32, "ind": False, "off": []}

    def c1(name, k):
        return v(name, R[k:k + 1])

    def ind(name, off, width=W):
        x = v(name, R[0:width])
        return dict(x, ap=x["ap"].indirect(off["ap"]), n=16 * off["n"], ind=True, off=off["k"])

    def u(x):
        return v(x) if isinstance(x, str) else x

    def raw(x):
        return x["ap"] if isinstance(x, dict) else x

    def op(e, f, outs, ins, c, sem=None, n=16, lat=0.0, far=False):
        r, w, banks = [], [], set()
        for x in [y for y in ins if isinstance(y, dict)] + outs:
            r.extend(x["off"])
            if x["ps"]:
                banks.add(x["k"][0][0])
            if not (x["ps"] and e == "P"):
                (w if any(x is y for y in outs) else r).extend(x["k"])
        ops.append({"e": e, "f": f, "r": r, "w": w, "x": sorted(banks), "tag": tag[0], "c": c, "sem": sem, "n": n, "lat": lat, "far": far,
                    "free": False, "sum": None, "stop": [False]})

    def cost(e, out, a, per):
        if out["ind"] or a["ind"]:
            return 0.06 + a["n"] * (SCA if out["ind"] else GA) * CY
        return max(64, a["n"] * per) * CY + (0.05 if e == "S" else 0.0)

    def dma(e, out, in_, lat):
        outs = [out] if isinstance(out, dict) else []
        op(e, lambda q: q.dma_start(raw(out), raw(in_)), outs, [in_], 0.1, "d%d" % ndma[0], 16, lat)
        ndma[0] += 1

    def ms(out, c):
        out = u(out)
        op("V", lambda q: q.memset(out["ap"], c), [out], [], cost("V", out, out, 0.5 if out["two"] else 1))

    def cp(out, a):
        out, a = u(out), u(a)
        op("V", lambda q: q.tensor_copy(out["ap"], a["ap"]), [out], [a], cost("V", out, a, 0.5 if out["two"] and a["two"] else 1))

    def tt(out, a, b, o):
        out, a, b = u(out), u(a), u(b)
        op("V", lambda q: q.tensor_tensor(out["ap"], a["ap"], b["ap"], o), [out], [a, b], cost("V", out, a, 1 if a["ps"] or b["ps"] else 2))

    def ts(out, a, s1, o0, s2=None, o1=None):
        out, a = u(out), u(a)
        args = (out["ap"], a["ap"], raw(s1), raw(s2), o0) + (() if o1 is None else (o1,))
        op("V", lambda q: q.tensor_scalar(*args), [out], [a, s1, s2], cost("V", out, a, 0.5 if out["two"] and a["two"] else 1))

    def red(out, a):
        a = u(a)
        op("V", lambda q: q.tensor_reduce(out["ap"], a["ap"], AxisListType.X, A.add), [out], [a], cost("V", out, a, 1))

    def scan(out, a, b, init, o0, o1):
        out, a, b = u(out), u(a), u(b)
        op("V", lambda q: q.tensor_tensor_scan(out["ap"], a["ap"], b["ap"], init, o0, o1), [out], [a, b], cost("V", out, a, 1))

    def act(out, a, fn=F.Identity, acc=None, **k):
        out, a = u(out), u(a)
        kw = {x: raw(y) for x, y in k.items()}
        if acc:
            kw["accum_out"] = acc["ap"]
        op("S", lambda q: q.activation(out["ap"], a["ap"], fn, **kw), [out] + ([acc] if acc else []), [a] + list(k.values()), cost("S", out, a, 1))

    def shift(e, out, a, c):
        if e == "S":
            act(out, a, bias=c)
        else:
            ts(out, a, c, A.add)

    def mm(out, *terms, st=True, sp=True, hold=False, run=False):
        terms = [(u(x[0]), u(x[1]), x[2] if len(x) > 2 else out) for x in terms]
        bank = terms[0][2]["k"][0][0]
        runs = [terms] if run else [[x] for x in terms]
        for j, xs in enumerate(runs):
            a, b = st and j == 0, [False]
            sums[bank] = sums.get(bank, 0) + a

            def f(q, xs=xs, a=a, b=b):
                return [q.matmul(o["ap"], l["ap"], rr["ap"], a and k == 0, b[0] and k == len(xs) - 1) for k, (l, rr, o) in enumerate(xs)][-1]
            op("P", f, [xs[0][2]], [y for x in xs for y in x[:2]], sum(max(64, rr["n"]) * (4 if l["f32"] else 1) * PE for l, rr, o in xs))
            ops[-1].update({"free": not a and not (hold and j == len(runs) - 1), "sum": (bank, sums[bank]), "stop": b})

    def iota(out, pat, base, cm=0):
        out = u(out)
        kw = {"allow_small_or_imprecise_dtypes": True} if out["two"] or out["f32"] else {}
        op("G", lambda q: q.iota(out["ap"], pat, base, cm, **kw), [out], [], 0.13 + 2 * out["n"] * CY)

    def sel(out, a, pat, o, base, cm, fill=0.0):
        out, a = u(out), u(a)
        op("G", lambda q: q.affine_select(out["ap"], a["ap"], pat, o, fill, base, cm), [out], [a], 0.17 + 2 * out["n"] * CY)

    col = [c1("col", k) for k in range(8)]
    M16, ONE = v("M16", R[0:128]), v("ONE", R[0:128])
    Q = v("BO", R[0:128:16])

    dma("Y", v("TN"), T.ts[:], 2.2)
    dma("S", v("L", 0), T.ts[0:8:2, :], 2.4)
    dma("Y", v("L", 1), T.ts[1:8:2, :], 2.6)
    dma("S", v("z0"), T.zq[:], 2.7)
    dma("Y", c1("kapi", 0), T.kap[:], 2.7)
    dma("S", v("thr", p=R[0:1]), T.th[:], 2.7)
    dma("Y", v("X", R[0:2048]), T.xr[:, 0:2048], 4.5)
    dma("Y", v("X", R[2048:V]), T.xr[:, 2048:V], 6.5)

    cp("Wn", "TN")
    t = 0
    for k in PLACE:
        for j in range(t, t + k):
            iota(v("VAL", R[512 * j:512 * j + 512]), [[1, 32], [256, 16]], 56 + 32 * j)
        act(ind("POS", v("Wn", R[32 * t:32 * (t + k)]), V), v("VAL", R[512 * t:512 * (t + k)]), F.Silu)
        t += k
    for t in range(t, 8):
        ts(ind("POS", v("Wn", R[32 * t:32 * t + 32]), V), v("VAL", R[0:512]), 1.0, A.mult, 32.0 * t, A.add)

    ms("ONE", 1.0)
    for n, c in (("HP", 0.5), ("NO1", -1.0), ("CT", 0.0), ("C2K", 2048.0)):
        ms(n, c)
    ms(v("FR", R[0:256]), 0.0)
    for k in (256, 512, 1024):
        act(v("FR", R[k:2 * k]), v("FR", R[0:k]))
    for k in range(2, 4):
        ms(v("FR", R[1024 * k:1024 * k + 1024]), 0.0)
    ms("ZE", 0.0)
    iota("mi", [[0, 8], [-1, 16]], 128, 1)
    sel("tmp", ONE, [[-16, 8], [0, 16]], A.is_ge, 0, 1)
    sel("BO", "tmp", [[16, 8], [0, 16]], A.is_ge, 15, -1)
    sel("ID", ONE, [[-1, 128]], A.is_equal, 0, 1)
    iota(v("CT", R[0:16:2]), [[1, 8]], 1)
    iota(v("CT", R[1:14:2]), [[-1, 7]], 7)
    iota(c1("CT", 15), [[0, 1]], 1)
    iota(v("CT", R[16:32]), [[0, 2], [1, 8]], 0)
    iota(v("CT", R[32:48]), [[1, 16]], 0)
    ts("q0", "mi", 15, A.bitwise_and)
    for k in range(2):
        ts(v("M16", R[128 * k:128 * k + 128]), "q0", 0.0, A.is_equal)
    tt(v("PRD", R[0:48]), v("CT", R[0:48]), v("M16", R[0:48]), A.mult)
    for k in range(3):
        red(col[k], v("PRD", R[16 * k:16 * k + 16]))
    ts(col[3], col[1], 8196.5, A.add)
    if "S" in (REPC, REPN):
        iota(v("rr", R[0:32]), [[16, 8], [0, 4]], 0)
        ts("oZ", v("rr", R[0:32]), col[2], A.add)
    for t in range(8):
        iota(v("VID", R[512 * t:512 * t + 512]), [[1, 512]], 512 * t)
    ms(c1("ac", 0), -0.375)
    cp("I32", "ID")
    cp(c1("cc", 0), c1("kapi", 0))
    ts("tmp", M16, c1("cc", 0), A.mult)
    cp("S0", "BO")
    mm(v("pD", R[0:128]), ("S0", "tmp"))
    cp("KAP", v("pD", R[0:128]))
    a, b = v("thb"), v("thr", p=R[0:1])
    op("G", lambda q, a=a, b=b: q.partition_broadcast(a["ap"], b["ap"], 128), [a], [b], 0.2)
    both = "".join(CANDS), "".join(NODES)
    for n, c, need in (("Z1", 32768.0, True), ("Z1n", -32768.0, "B" in both[0]), ("Z2", -8192.0, True), ("Z2b", -16384.0, "B" in both[1]), ("Z2p", 8192.0, "B" in both[1])):
        if need:
            iota(n, [[0, 144]], 0)
            ts(v(n, R[15:128:16]), Q, c, A.mult)
    for n, c in (("NI", -1.0), ("HI", 0.5), ("NHI", -0.5), ("I64", 64.0), ("N64", -64.0), ("IX", 32.0), ("IT", -2.0 ** -11), ("NB", -2.0 ** 23),
                 ("IA", 1032.0 * 8192), ("IB", -2040.0 * 8192))[:10 if "B" in both[1] else 8]:
        sel(n, "ZE", [[-1, 128]], A.not_equal, 0, 1, c)
    for n, c in (("MA", -1664.0), ("MB", 2047.0)):
        ts(n, M16, c, A.mult)
    WB = v("RX", R[0:128])
    for n, c in ((WB, 1.0), (v("RX", R[128:256]), 0.0625)):
        ts(n, "BO", col[0], A.mult, c, A.mult)
    for n, c in (("RS", 2.0 ** -4), ("RN", 2.0 ** -18)):
        ts(n, "BO", c, A.mult)
    for n, c in (("CK", -504 * 32768), ("CP", -10304), ("C19", 2 ** 19), (v("CU", R[0:128]), -2047), (v("CU", R[128:256]), 1536),
                 ("PV0", V + 56), ("PV1", V + 184)):
        iota(n, [[1 if n in ("PV0", "PV1") else 0, 128]], c)
    for n, c in (("CF", -15 / 32.0), ("CH", 63.75)):
        ms(n, c)
    ts("WQ", Q, 32.0, A.mult)
    for k in range(8):
        ts(v("SELG", k), ONE, c1("WQ", k), A.mult)
    ts("SELN", "SELG", -1.0, A.mult)
    iota(c1("cc", 2), [[0, 1]], 0, 1)
    ts("Q32", Q, 16384.0, A.mult)
    ts("QA", Q, 4096.0, A.mult)
    ts("QB", Q, c1("cc", 2), A.mult)
    iota(v("dc", R[0:2]), [[128, 2]], V + 8256, 1)
    ts(v("dc", R[2:4]), v("dc", R[0:2]), 512.0, A.mult)
    ts(c1("dc", 4), c1("cc", 2), 2.0 ** -14, A.mult, 0.25, A.add)
    ts(c1("dc", 5), c1("dc", 4), 2.0 ** -7, A.add)
    for k in range(2):
        ts(v("DMP", R[128 * k:128 * k + 128]), M16, c1("dc", 4 + k), A.mult)
    ts(c1("cc", 7), c1("cc", 2), 16.0 * SCR, A.is_ge, 64.0, A.mult)
    tt(c1("cc", 6), c1("cc", 7), col[2], A.add)
    for j, (s, base) in enumerate(((0, 1), (-1, 0), (16, 0))):
        iota(v("KW", j), [[s, 32]], base)
        iota(v("KQ", j), [[s, 4], [4 * s, 2], [8 * s, 4]], base)
    for k in range(8):
        ts(v("TW", R[:, :, k]), "KW", c1("BO", 16 * k), A.mult)
        ts(v("TQ", R[:, k]), "KQ", c1("BO", 16 * k), A.mult)
    for n, c, step, start in (("RST", 0, 32, -1e9), ("RSC", -2048, 16, 1e9)):
        iota(n, [[0, 256]], c)
        ms(v(n, R[0:256:step]), start)
    iota("r1", [[0, 8], [1, 16]], 0)
    iota("IOC", [[1, 264]], -1)
    iota("TA", [[0, 128]], -256)
    sel("TA", "TA", [[-1, 128]], A.is_gt, 0, 1)
    sel("TRI", ONE, [[1, 128]], A.is_gt, 0, -1)
    ms(v("A0", 0), 0.0)
    for k in (1, 2, 4):
        dma("Y", v("A0", R[k:2 * k]), v("A0", R[0:k]), 2.5)
    dma("Y", v("A1"), v("A0"), 2.5)
    dma("Y", v("X", R[V:W]), v("ZE"), 2.0)
    for n, w in (("XA", WX), ("XB", WX), ("POS", W)):
        dma("Y", v(n, R[V:w]), v("RSC", R[0:w - V]), 2.0)
    ts("osf", Q, 1.0, A.mult)
    tt("plf", "thb", "osf", A.mult)
    red(c1("cc", 1), "plf")
    ts(c1("th", 0), c1("cc", 1), 0.5, A.add)
    ts(c1("th", 3), c1("cc", 1), 64.5, A.add)

    for g0 in range(2):
        cp(v("M", R[:, 16 * g0:16 * g0 + 16]), v("L", g0))
    a, b = v("Mt"), v("M")
    op("V", lambda q, a=a, b=b: q.transpose(a["ap"], b["ap"]), [a], [b], 256 * CY)
    for c in range(8):
        cp(v("Wu", R[c:256:8]), v("Mt", c))
    ts("TF", "TN", 2.0 ** -14, A.mult)
    ts("DH", "TN", 2.0 ** -14, A.mult)
    mm(v("pE", R[0:256]), ("I32", "TF"), ("NI", "DH"))
    cp("DL", v("pE", R[0:256]))
    dma("Y", v("FR", p=R[0:128:16]), v("DH"), 2.0)
    dma("Y", v("FR", p=R[1:128:16]), v("DL"), 2.0)
    tag[0] = "first"
    for t in range(8):
        cols = R[512 * t:512 * t + 512]
        tt(v("XA", cols), ind("X", v("Wu", R[32 * t:32 * t + 32]), V), v("FR", cols), A.add)
    tag[0] = None

    my = masks(topo, core, T.cores)
    arrive = sum(len(masks(topo, c, T.cores)[core]) for c in T.cores if c != core)
    XT = ["XA", "XB", "XA"]
    blk = lambda b: R[16 * b:16 * b + 16]

    def piece(c, n):
        return v("pK", R[n // 2 * (c % 2) + c // 2:32 * n:n])

    def repeat(engines, src, c):
        if engines == "S":
            act("REP", ind(src, v("oZ"), 128), bias=c)
            return
        for k in range(4):
            shift(engines[k], v("RP4", R[:, k]), src, c)
        cp("REP", "RP4")

    def measure(c, hows, win, off, bias, zz):
        how = hows[c]
        for a, b in ((0, 5), (5, 8)) if HALF and c == len(hows) - 1 and how == "A" else ((0, 8),):
            d, size = v("D", R[512 * c + 64 * a:512 * c + 64 * b]), v("AB", R[8 * (c // 2) + a:8 * (c // 2) + b, :, c % 2])
            src = ind(win, v(off, R[32 * c + 4 * a:32 * c + 4 * b]))
            if how == "C":
                bank = v(("pA", "pB")[turn[0] % 2], R[64 * a:64 * b])
                turn[0] += 1
                act(d, src, bias=bias)
                mm(bank, ("NI", v("REP", R[64 * a:64 * b])), ("ID", d))
                act(size, bank, F.Abs, bias=-2 * bias)
                continue
            tt(d, src, v("REP", R[64 * a:64 * b]), A.subtract)
            if how == "A":
                act(size, d, F.Abs, bias=-bias)
            elif bias:
                ts(size, d, -bias, A.add, 0.0, A.max)
            else:
                ts(size, d, 0.0, A.max, 2.0, A.mult)
        b, n = c // 2, len(hows)

        def add(out, z, rhs):
            mm(out, *[(v(z, R[15 - r:143 - r]), rhs(r)) for r in range(16)], st=False, run=True)
        tag[0] = ("pair", b) if bias and "B" in hows[2 * b:2 * b + 2] else None
        if how == "B":
            add(piece(c, n), zz[2], lambda r: v("D", R[512 * c + r:512 * c + 512:16]))
        if (hows[2 * b] == "B") != (hows[2 * b + 1] == "B"):
            add(piece(c, n), zz[how == "B"], lambda r: v("AB", R[8 * b:8 * b + 8, :, c % 2, r]))
        elif c % 2:
            add(v("pK", R[b:32 * n:n // 2]), zz[how == "B"], lambda r: v("AB", R[8 * b:8 * b + 8, :, :, r]))
        tag[0] = None

    def reorder(src, dst, lst, on_s):
        t = 0
        while t < 16:
            s = t >= 16 - on_s
            k = min(STEP_S if s else STEP_V, (16 if s else 16 - on_s) - t)
            tag[0] = "move"
            (act if s else cp)(v(dst, R[256 * t:256 * (t + k)]), ind(src, v(lst, R[16 * t:16 * (t + k)])))
            tag[0] = None
            t += k

    def cands(rd, zb):
        ut = v("pA", R[0:128])
        mm(ut, ("NI", "C2K"), (zb, WB))
        tt("um", ut, M16, A.mult)
        for b in ("pB", "pC"):
            mm(v(b, R[0:128]), ("ID", "C2K"), ("um", "BO"))
        keys = v("pK", R[0:128])
        mm(keys, ("ID", "CK"), sp=False)
        repeat(REPC, zb, 0.0)
        act("uu", v("pB", R[0:128]), F.Square)
        tt(v("pC", R[128:256]), v("pC", R[0:128]), "KAP", A.mult)
        ts("q0", "uu", 0.03125, A.mult, c1("ac", rd), A.add)
        tt("sum", v("pC", R[128:256]), "q0", A.add)
        ts("h", "sum", V - 1, A.bitwise_and)
        for c in range(4):
            cp(v("oC", R[32 * c:32 * c + 32]), v("h", R[:, 2 * (c % 2) + c // 2:16:4]))
            measure(c, CANDS[rd], "X", "oC", 0.0, ("Z1", "Z1", "Z1n"))
        ts("PB", "h", 2048.0, A.max, -2048.0, A.add)
        ts("PA", "h", 2048.0, A.min)
        tt(v("KA", R[0:128]), keys, "PA", A.subtract)
        tt(v("KA", R[128:256]), keys, "PB", A.add)
        scan("KS", "RSC", "KA", 0.0, A.add, A.min)
        tt("sW", v("KS", R[143:256:16]), v("KS", R[15:128:16]), A.subtract)
        cp(v("su", R[0:8]), "sW")

    def bank4(k):
        return v("pS%d" % (k // 4), R[128 * (k % 4):128 * (k % 4) + 128])

    def pairs(digits):
        for b in range(2):
            ks = range(4 * b, 4 * b + 4)
            mm(None, *[("ID", "TRI", bank4(k)) for k in ks], run=True)
            mm(None, *[x for k in ks for x in ((v("SELG", k), digits, bank4(k)), (digits, v("SELN", k), bank4(k)))], st=False, run=True)

    def by_group(bank, buf, rhs, at=0):
        for b in range(2):
            mm(None, *[(v(buf, k), v(rhs, R[16 * k:16 * k + 16]), v(bank, R[at + 16 * k:at + 16 * k + 16])) for k in range(4 * b, 4 * b + 4)], st=False, run=True)

    def places(rd):
        sl, P = v("su", R[0:8]), v("pA", R[0:128])
        ts("pd", ind("POS", sl), col[3], A.add)
        act("xs", ind("X", sl))
        n1, n2, n3, kn = v("pC", R[0:64]), v("pE", R[0:192]), v("pE", R[192:200]), v("pK", R[0:256])
        tw = lambda j, a, b: v("TW", R[j, a // 32:b // 32])
        tq = lambda j: v("TQ", j)
        mm(n1, ("MA", tw(2, 0, 64)), ("MB", tw(0, 0, 64)), sp=False)
        mm(n2, ("MA", tw(2, 64, 256)), ("MB", tw(0, 64, 256)), sp=False)
        mm(n3, ("MB", Q), (M16, Q), st=False, sp=False)
        mm(kn, ("MA", tq(2)), ("MB", tq(0)), sp=False)

        mm(v("pB", R[0:256]), ("ID", "CU"), sp=False)
        mm(v("pB", R[128:256]), ("ID", "CF"), st=False, sp=False)
        mm(v("pB", R[0:256]), ("xs", "RX"), st=False)
        mm(P, ("ID", "CP"), sp=False)
        if rd:
            mm(v("pA", R[16 * SGR:128]), *[("HP", v("NO1", R[16 * SGR:128]))] * rd, st=False, sp=False)
            for b in (1, 0):
                mm(None, *[(v("SELG", k), "pd", bank4(k)) for k in range(4 * b, 4 * b + 4)], run=True)
        mm(P, ("pd", "RS"), st=False, sp=rd == 0)
        repeat(REPN, "xs", -192.0)
        for s in range(rd):
            buf = ("GT", "GU")[s]
            for k in range(8):
                if k < SGR:
                    ts(v(buf, k), bank4(k), c1("RT%d" % s, k), A.is_gt)
                else:
                    act(v(buf, k), bank4(k), F.Sign, scale=-1.0, bias=c1("RT%d" % s, k))
            for k0 in range(0, 8, 2):
                mm(None, *[(v(buf, k), v("NO1" if k < SGR else "HP", R[0:16]), v("pA", R[16 * k:16 * k + 16])) for k in (k0, k0 + 1)], st=False, run=True)
        tt("UF", v("pB", R[0:256]), "M16", A.mult)
        tt("Pm", P, M16, A.mult)
        Um, Fm = v("UF", R[0:128]), v("UF", R[128:256])
        mm(n1, (Um, tw(1, 0, 64)), (Fm, tw(2, 0, 64)), ("Pm", tw(0, 0, 64)), st=False)
        mm(n2, (Um, tw(1, 64, 256)), (Fm, tw(2, 64, 256)), ("Pm", tw(0, 64, 256)), st=False, sp=False)
        mm(n3, ("Pm", Q), st=False)
        mm(kn, (Um, tq(1)), (Fm, tq(2)), ("Pm", tq(0)), st=False, hold=True)
        if "B" in NODES[rd]:
            mm(None, *[("IB" if NODES[rd][c] == "B" else "IA", v("ONE", R[0:32]), piece(c, 8)) for c in range(8)], st=False, hold=True, run=True)
        cp(v("oN", R[0:64]), n1)
        cp(v("oN", R[64:264]), v("pE", R[0:200]))
        act("pT", P, scale=-256.0)

    def match(rd, zb):
        d0, d1, d2, d3 = (v("pD", R[128 * k:128 * k + 128]) for k in range(4))
        mm(d0, ("ID", zb), ("NI", "xs"))
        act("ad", d0, F.Abs)
        mm(d2, ("BO", "ad"))
        act("sg", d2, F.Sign, c1("cc", 5), scale=-1.0, bias=c1("th", rd))
        if rd < 2:
            act(c1("ac", rd + 1), c1("cc", 5), scale=-0.5, bias=63.625)
            act(c1("th", rd + 1), c1("cc", 5), scale=-0.5, bias=c1("th", 3))
        mm(d3, ("sg", "ID"))
        act("mt", d3, F.Relu)
        mm(d1, ("NHI", "HP"), ("HI", zb), ("HI", "xs"), run=True)
        ts("c2", d0, -2.0, A.max, 2.0, A.min)
        ts("vs", d1, MAGIC, A.add, -MAGIC, A.add)
        tt("fs", ind(XT[rd], v("oN", R[256:264])), "xs", A.subtract)
        pairs("pd")
        for b in range(2):
            ts(v("Y", R[4 * b:4 * b + 4]), v("pS%d" % b), 0.0, A.max, 256.0, A.min)
        mm(d0, ("HI", ONE), ("sg", "NHI"), run=True)
        by_group("pD", "Y", "mt")
        ts("rr", d0, 256 * MAGIC, A.add, -256 * MAGIC, A.add)
        tt("first", d0, "rr", A.is_equal)
        tt("nfm", "first", M16, A.is_lt)
        w = v("pD", R[128:136])
        mm(w, ("nfm", "QA"), ("nfm", "QB"))
        tt("osf", w, "sW", A.max)
        cp(v("oS", R[0:8]), "osf")
        if rd < 2:
            w = v("pD", R[136:144])
            mm(w, ("NB", v("NO1", R[0:8])), ("pd", "WQ"), ("NB", v("first", R[0:128:16])))
            ts("RT%d" % rd, w, c1("dc", 2 + rd), A.min)
            act(ind("POS", v("oS", R[0:8])), "PV%d" % rd, F.Silu)
        a, b = v("pC", R[0:128]), v("pC", R[128:256])
        mm(b, ("ID", "C19"), ("ID", "C19"), (ONE, ONE), ("ID", "C19", a), ("I32", "pT", a), run=True)
        mm(b, ("TA", "first"), ("TA", "first", a), st=False, run=True)
        by_group("pC", "Y", "first")
        tt("ww", a, "first", A.mult)
        tt("ti", b, "ww", A.subtract)
        if SCR < 8:
            ts("ntc", v("ti", R[0:128:16]), -2.0 ** -12, A.mult, 1.0, A.add)
        if SCR:
            ts("tc", v("ti", R[0:128:16]), 2.0 ** -12, A.mult, -1.0, A.add)
        ts("tr", "ti", 8, A.arith_shift_right, 15, A.bitwise_and)
        for k in range(8):
            if k < SCR:
                ts(v("SC", R[k, 0:257]), v("IOC", R[0:257]), c1("tc", k), A.is_ge, 2.0, A.mult)
            else:
                act(v("SC", R[k, 0:257]), v("IOC", R[0:257]), F.Sign, bias=c1("ntc", k))
        tt(v("A1", R[:, 112:128]), "tr", "r1", A.is_le)
        ts(v("A0", R[:, 112:128]), v("A1", R[:, 112:128]), -1.0, A.mult, 1.0, A.add)
        mm(v("pE", R[0:256]), ("IX", v("IOC", R[1:257])))
        for k in range(8):
            mm(v("pE", R[0:256]), (v("A1", R[k, 112 - 16 * k:240 - 16 * k]), v("SC", R[k, 1:257])),
               (v("A0", R[k, 112 - 16 * k:240 - 16 * k]), v("SC", R[k, 0:256])), st=False, run=True)
        ts("oR", v("pE", R[0:256]), 0.5, A.mult, c1("cc", 6), A.add)

    def nodes(rd, zb):
        xt = XT[rd]
        for c in range(8):
            measure(c, NODES[rd], xt, "oN", 192.0, ("Z2", "Z2b", "Z2p"))
        scan("KS", "RST", v("pK", R[0:256]), 0.0, A.add, A.max)
        ts("ki", v("KS", R[31:256:32]), 512.0, A.add)
        ts("kj", "ki", 8191, A.bitwise_and)
        pl = v("pu", R[0:8])
        ts(pl, "kj", -512.0, A.add)
        win = ind(xt, pl)
        sn, ln = "send%d" % rd, "land%d" % rd
        a, b, c = v("pA", R[0:128]), v("pB", R[0:128]), v("pB", R[128:256])
        ts("xn", win, MAGIC, A.add, -MAGIC, A.add)
        mm(a, (ONE, "HP"), ("NI", zb), ("I64", "sg"), ("ID", "xn"))
        mm(b, ("ID", "CH"), ("HI", zb), ("N64", "sg"), ("HI", "xn"))
        act("r2", a, F.Abs)
        ts(c, b, MAGIC, A.add, -MAGIC, A.add)
        tt(sn, c, "r2", A.min)
        trs, lands = [], []
        for c, e in my.items():
            rid, pid, _ = topo.addr(c)
            b = T.rank_of(c)
            lands.append(v(ln, blk(b)))
            trs.append(RemoteDMATransfer(dst_ids=[DstId(rid=rid, pnc=pid)], dma_engine_mask=sum(1 << x for x in e), remote_sem=T.sem["arr%d" % rd],
                                         src=v(sn, blk(b))["ap"], dst=v(ln, blk(rank))["ap"]))
        op("G", lambda q: q.remote_dma_fused(trs, local_sem=T.sem.sent), lands, [v(sn)], 0.5, "arr%d" % rd, arrive, 3.0, True)
        act(v(ln, blk(rank)), v(sn, blk(rank)))
        ts("pn", ind("VID", pl, V), col[3], A.add)
        tt("fr", win, "xn", A.subtract)

    def near(rd):
        n = 2 if rd < 2 else 1
        pairs("pn")
        mm(v("pK", R[256:384]), ("ID", "c2"), ("ID", "xn"))
        ts("vn", v("pK", R[256:384]), 0.0, A.max, 63.0, A.min)
        for b in range(2):
            ts(v("EQ", R[4 * b:4 * b + 4]), v("pS%d" % b), 1.0, A.is_equal)
        mm(v("pD", R[0:128]), ("HI", ONE), ("fr", "BO"), sp=False)
        if rd < 2:
            mm(v("pD", R[128:256]), ("IT", ONE), ("pn", "RN"), st=False, sp=False)
        for j in range(n):
            mm(v("pD", R[128 * j:128 * j + 128]), ("sg", "NHI"), st=False)
            by_group("pD", "EQ", "mt", 128 * j)
        tt(v("sn", R[0:128 * n]), v("pD", R[0:128 * n]), v("DMP", R[0:128 * n]), A.min)
        mm(None, *[(v("sn", R[128 * j:128 * j + 128]), "Q32", v("pD", R[256 + 8 * j:264 + 8 * j])) for j in range(n)], run=True)
        cp(v("oT", R[0:8 * n]), v("pD", R[256:256 + 8 * n]))
        a, b = v("pK", R[384:512]), v("pA", R[128:256])
        if rd < 2:
            mm(a, ("ID", "vn"), ("ID", "fr"))
            act("nv", a)
            mm(b, ("ID", "vs"), ("ID", "fs"))
            act(v(XT[rd], R[V:W]), b)
            cp(ind(XT[rd], v("oT", R[8:16]), WX), "nv")
        cp(ind("X", v("oT", R[0:8])), "vn")
        cp(ind("X", v("oS", R[0:8])), "vs")

    for rd in range(3):
        zb = "z0" if rd == 0 else "land%d" % (rd - 1)
        cands(rd, zb)
        places(rd)
        if rd == 2:
            for k in range(2):
                dma("Y", v("seg", R[256 * k:256 * k + 256]), v("XA", R[0:V], p=R[k:128:16]), 2.5)
            act("sega", "seg", bias=192.0)
            w = v("pE", R[256:512])
            mm(w, *[x for k in range(2) for x in (("I32", v("seg", R[256 * k:256 * k + 256])), ("NI", v("sega", R[256 * k:256 * k + 256])))])
            act("Wf", w, scale=16384.0, bias=384.0 * 16384)
            dma("Y", v("XB", R[0:V], p=R[0:128:16]), v("Wf"), 2.5)
        match(rd, zb)
        if rd == 2:
            w = v("pD", R[256:384])
            mm(w, ("BO", "fs"))
            act(v("XB", R[V:W]), w, scale=16384.0)
            reorder("XB", "POS", "oR", LAST_S)
            dma("Y", T.yt[:], v("POS", R[0:V], p=R[0:128:16]), 2.5)
        nodes(rd, zb)
        near(rd)
        if rd < 2:
            reorder(XT[rd], XT[rd + 1], "oR", MOVE_S)
    dma("Y", T.yx[:, 0:2048], v("X", R[0:2048]), 4.5)
    dma("S", T.yx[:, 2048:V], v("X", R[2048:V]), 5.0)
    dma("Y", T.yz[:], v("land2"), 2.0)
    emit(g, T, arrange(ops))
    g.wait_ge(T.sem.sent, 3 * sum(len(e) for e in my.values()))
